import numpy as np
import ml_dtypes


def mxq(x, axis, fmt="e4m3"):
    dtype, down = {"e4m3": (ml_dtypes.float8_e4m3fn, 7), "e5m2": (ml_dtypes.float8_e5m2, 14)}[fmt]
    v = np.moveaxis(np.asarray(x, np.float32).astype(ml_dtypes.bfloat16).astype(np.float64), axis, -1)
    blocks = v.reshape(v.shape[:-1] + (-1, 32))
    amax = np.abs(blocks).max(-1, keepdims=True)
    byte = np.maximum(np.where(amax > 0, np.frexp(amax)[1] - 1 + 127, 0) - down, 1)
    scale = np.exp2(byte - 127.0)
    codes = (blocks / scale).astype(np.float32).astype(dtype).astype(np.float64)
    return np.moveaxis((codes * scale).reshape(v.shape), -1, axis)


WIDE = False


def mx_kscale(k):
    if not WIDE:
        return np.ones(k)
    levels = np.array([10, -10, 5, -5, 0])
    if k % 512:
        return np.exp2(np.random.permutation(np.resize(levels, k // 32))).repeat(32)
    a = np.empty((k // 512, 16))
    for p in range(k // 512):
        a[p, :8] = np.random.permutation(np.resize(levels, 8))
        for g in range(8):
            far = levels[np.abs(levels - a[p, g]) >= 10]
            a[p, g + 8] = far[np.random.randint(len(far))]
    return np.exp2(a.ravel()).repeat(32)


def f64(x):
    return np.asarray(x).astype(np.float64)


def striped(idx):
    return np.tile(idx.reshape(-1, 16).T, (8, 1)).astype(np.uint16)


def unstriped(offs):
    return offs[:16].T.reshape(-1).astype(np.int64)


def striped8(idx):
    return np.concatenate([x.reshape(-1, 16).T for x in idx]).astype(np.uint16)


def runs(offs, k):
    lists = np.stack([offs[16 * r : 16 * r + 16].T.reshape(-1) for r in range(8)]).astype(np.int64)
    return lists[np.arange(k) % 512 // 64]


def pack_weight(w):
    k, n = w.shape
    w = f64(np.asarray(w, np.float32).astype(ml_dtypes.bfloat16)).reshape(k // 32, 32, n)
    amax = np.abs(w).max(1)
    byte = np.clip(np.where(amax > 0, np.frexp(amax)[1] - 1 + 127 - 7, 1), 1, 254)
    scaled = (w * np.exp2(127.0 - byte)[:, None, :]).reshape(k, n).astype(np.float32)
    words = np.ascontiguousarray(scaled.reshape(k // 512, 128, 4, n).transpose(0, 1, 3, 2)).astype(ml_dtypes.float8_e4m3fn).view(np.uint8)
    return words, np.ascontiguousarray(byte.astype(np.uint8).reshape(k // 512, 16, n))


def unpack_weight(words, scales):
    g, p, n, _ = words.shape
    vals = np.ascontiguousarray(words).view(ml_dtypes.float8_e4m3fn).astype(np.float64) * np.repeat(np.exp2(scales.astype(np.float64) - 127.0), 8, axis=1)[..., None]
    return vals.transpose(0, 1, 3, 2).reshape(g * 512, n)


E2M1 = np.array([0.0, 0.5, 1.0, 1.5, 2.0, 3.0, 4.0, 6.0, -0.0, -0.5, -1.0, -1.5, -2.0, -3.0, -4.0, -6.0])


def pack_fp4(w):
    k, n = w.shape
    w = f64(np.asarray(w, np.float32).astype(ml_dtypes.bfloat16)).reshape(k // 32, 32, n)
    amax = np.abs(w).max(1)
    mant, ex = np.frexp(amax / 6.0)
    byte = np.clip(np.where(amax > 0, np.where(mant > 0.5, ex, ex - 1) + 127, 1), 1, 254)
    scaled = (w * np.exp2(127.0 - byte)[:, None, :]).reshape(k, n).astype(np.float32)
    c = np.ascontiguousarray(scaled.reshape(k // 512, 128, 4, n).transpose(0, 1, 3, 2)).astype(ml_dtypes.float4_e2m1fn).view(np.uint8) & 0xF
    words = (c[..., 0::2] | (c[..., 1::2] << 4)).reshape(k // 512, 128, 2 * n)
    return np.ascontiguousarray(words), np.ascontiguousarray(byte.astype(np.uint8).reshape(k // 512, 16, n))


def unpack_fp4(words, scales):
    g, _, n = scales.shape
    words = np.ascontiguousarray(words).reshape(g, 128, n, 2)
    nib = np.empty((g, 128, n, 4), np.uint8)
    nib[..., 0::2] = words & 0xF
    nib[..., 1::2] = words >> 4
    vals = E2M1[nib] * np.repeat(np.exp2(scales.astype(np.float64) - 127.0), 8, axis=1)[..., None]
    return vals.transpose(0, 1, 3, 2).reshape(g * 512, n)


def silu(v):
    return v / (1.0 + np.exp(-np.maximum(v, -700.0)))

def planes(y):
    n, m = y.shape
    v = y.astype(np.float32).astype(ml_dtypes.bfloat16).astype(np.float64).reshape(n // 32, 32, m)
    top = np.abs(v).max(1)
    byte = np.clip(np.where(top > 0, np.frexp(top)[1] - 1 + 127 - 7, 1), 1, 254)
    codes = (v * np.exp2(127.0 - byte)[:, None, :]).reshape(n, m).astype(np.float32).astype(ml_dtypes.float8_e4m3fn).view(np.uint8)
    words = codes.reshape(n // 512, 128, 4, m).transpose(0, 1, 3, 2)
    return np.ascontiguousarray(words), np.ascontiguousarray(byte.astype(np.uint8).reshape(n // 512, 16, m))


K, T, S, V, N, H = 512, 2048, 512, 256, 512, 512


def setup_inputs():
    n = np.random.standard_normal
    s = mx_kscale(K)[:, None]
    u = mx_kscale(H)
    packed_xT = pack_weight(n((K, T)) * s)
    packed_w2 = pack_fp4(n((H, N)) / np.sqrt(H) / u[:, None])
    return {
        "x_words": packed_xT[0],
        "x_scales": packed_xT[1],
        "w1": (n((K, H)) / np.sqrt(K) / s * u).astype(np.float32),
        "wt": np.repeat(np.random.uniform(0.3, 1.2, (8, V)), 64, axis=0).astype(np.float32),
        "w2_words": packed_w2[0],
        "w2_scales": packed_w2[1],
        "offs": striped(np.random.permutation(T)[:S]),
        "take": striped8(np.stack([np.random.permutation(S)[:V] for _ in range(8)])),
    }


def reference(x_words, x_scales, w1, wt, w2_words, w2_scales, offs, take):
    xq = unpack_weight(x_words, x_scales)[:, unstriped(offs)]
    y = mxq(f64(w1), 0, "e4m3").T @ xq
    e = (silu(y[np.arange(H)[:, None], runs(take, H)])) * f64(wt)
    z = y.copy()
    z[np.arange(H)[:, None], runs(take, H)] = e
    out_0 = unpack_fp4(w2_words, w2_scales).T @ mxq(z, 0, "e4m3")
    return (out_0,) + planes(out_0)

@@ -1,0 +1,171 @@
+from contextlib import ExitStack
+
+import concourse.mybir as mybir
+
+K, T, S, V, H, N = 512, 2048, 512, 256, 512, 512
+FLOPS = 2 * K * H * S + 2 * H * N * S
+BYTES = K * T + 16 * T + 4 * K * H + 4 * 8 * V + H * N // 2 + 16 * N + 2 * 128 * (S + V) // 16 + 4 * N * S + N * S + 16 * S
+
+F32 = mybir.dt.float32
+BF16 = mybir.dt.bfloat16
+I32 = mybir.dt.int32
+U32 = mybir.dt.uint32
+U16 = mybir.dt.uint16
+U8 = mybir.dt.uint8
+FP8X4 = mybir.dt.float8_e4m3fn_x4
+FP4X4 = mybir.dt.float4_e2m1fn_x4
+SILU = mybir.ActivationFunctionType.Silu
+MULT = mybir.AluOpType.mult
+
+P = 128
+PACK = 4
+QUADS = 4
+HALF = P // 2
+CH = 128
+NCH = S // CH
+
+
+def tile_picked_modtrue_silu_po_kernel(
+    tc, x_words, x_scales, w1, wt, w2_words, w2_scales, offs, take, out_0, out_1, out_2
+):
+    nc = tc.nc
+    with ExitStack() as ctx:
+        sb = ctx.enter_context(tc.tile_pool(name="sb", bufs=1))
+        ps = ctx.enter_context(tc.psum_pool(name="ps", bufs=1))
+
+        offs_t = sb.tile([P, S // 16], U16, name="offs_t")
+        take_t = sb.tile([P, V // 16], U16, name="take_t")
+        xw = sb.tile([P, T], U32, name="xw", align_bytes=64)
+        xs = sb.tile([P, T], U8, name="xs", align_bytes=64)
+        w2w = sb.tile([P, 2 * N], U8, name="w2w", align_bytes=64)
+        w2s = sb.tile([P, N], U8, name="w2s", align_bytes=64)
+        gate = sb.tile([P, V], F32, name="gate", align_bytes=64)
+        warm_in = sb.tile([P, 8], F32, name="warm_in")
+        warm_out = sb.tile([P, 8], F32, name="warm_out")
+        w1raw = [sb.tile([P, PACK, H // 2], F32, name=f"w1raw{h}", align_bytes=64) for h in range(2)]
+
+        nc.vector.memset(xs[:].bitcast(I32), 0)
+        nc.vector.memset(w2s[:].bitcast(I32), 0)
+        nc.vector.memset(warm_in[:], 0.0)
+
+        nc.sync.dma_start(offs_t[:], offs)
+        for q in range(QUADS):
+            nc.scalar.dma_start(xs[32 * q : 32 * q + 4, :].bitcast(I32), x_scales[0, 4 * q : 4 * q + 4, :].bitcast(I32))
+        nc.sync.dma_start(xw[:].bitcast(I32), x_words[0].rearrange("p c r -> p (c r)").bitcast(I32))
+        w1_rows = w1.rearrange("(p j) c -> p j c", j=PACK)
+        for h in range(2):
+            nc.sync.dma_start(w1raw[h][:], w1_rows[:, :, h * (H // 2) : (h + 1) * (H // 2)])
+        nc.sync.dma_start(take_t[:], take)
+        nc.sync.dma_start(gate[:], wt.rearrange("(p j) v -> p j v", j=PACK)[:, 0, :])
+        nc.sync.dma_start(w2w[:].bitcast(I32), w2_words[0].bitcast(I32))
+        for q in range(QUADS):
+            nc.sync.dma_start(w2s[32 * q : 32 * q + 4, :].bitcast(I32), w2_scales[0, 4 * q : 4 * q + 4, :].bitcast(I32))
+
+        nc.scalar.activation(warm_out[:], warm_in[:], SILU)
+
+        xsg = sb.tile([P, S], U8, name="xsg", align_bytes=64)
+        xwg = sb.tile([P, S], U32, name="xwg", align_bytes=64)
+        nc.vector.tensor_copy(xsg[:], xs[:].indirect(offs_t[:]))
+        nc.vector.tensor_copy(xwg[:], xw[:].indirect(offs_t[:]))
+
+        w1c = sb.tile([P, H], U32, name="w1c", align_bytes=64)
+        w1s = sb.tile([P, H], U8, name="w1s", align_bytes=64)
+        w1g = [sb.tile([P, PACK * HALF * PACK], BF16, name=f"w1g{h}", align_bytes=64) for h in range(2)]
+        for h in range(2):
+            dst = w1g[h][:].rearrange("p (t m j) -> p m t j", t=PACK, j=PACK)
+            src = w1raw[h][:].rearrange("p j (m t) -> p m t j", t=PACK)
+            if h == 0:
+                nc.scalar.copy(dst, src)
+            else:
+                nc.vector.tensor_copy(dst, src)
+            for t in range(PACK):
+                cols = slice(P * t + HALF * h, P * t + HALF * (h + 1))
+                nc.vector.quantize_mx(
+                    out=w1c[:, cols].bitcast(FP8X4),
+                    scales=w1s[:, cols],
+                    in_=w1g[h][:, t * HALF * PACK : (t + 1) * HALF * PACK],
+                )
+
+        z = []
+        for t in range(PACK):
+            cols = slice(P * t, P * (t + 1))
+            acc = ps.tile([P, S], F32, name=f"y_acc{t}")
+            nc.tensor.matmul_mx(
+                out=acc[:], lhsT=w1c[:, cols].bitcast(FP8X4), lhsT_scale=w1s[:, cols],
+                rhs=xwg[:].bitcast(FP8X4), rhs_scale=xsg[:], start=True, stop=True,
+            )
+            zt = sb.tile([P, S], F32, name=f"z{t}", align_bytes=64)
+            nc.scalar.copy(zt[:], acc[:])
+            z.append(zt)
+
+        w2wd = sb.tile([P, 2 * N], U8, name="w2wd", align_bytes=64)
+        w2sd = sb.tile([P, N], U8, name="w2sd", align_bytes=64)
+        nc.vector.tensor_copy(
+            w2wd[:].rearrange("p (t m b) -> p m t b", t=PACK, b=2), w2w[:].rearrange("p (m t b) -> p m t b", t=PACK, b=2)
+        )
+        nc.vector.tensor_copy(w2sd[:].rearrange("p (t m) -> p m t", t=PACK), w2s[:].rearrange("p (m t) -> p m t", t=PACK))
+
+        zq = [sb.tile([P, CH, PACK], BF16, name=f"zq{c}", align_bytes=64) for c in range(NCH)]
+        act = []
+
+        def gather(t):
+            g = sb.tile([P, V], F32, name=f"g{t}", align_bytes=64)
+            nc.vector.tensor_copy(g[:], z[t][:].indirect(take_t[:]))
+            a = sb.tile([P, V], F32, name=f"a{t}", align_bytes=64)
+            nc.scalar.activation(a[:], g[:], SILU)
+            act.append(a)
+
+        def scatter(t):
+            nc.vector.tensor_tensor(z[t][:].indirect(take_t[:]), act[t][:], gate[:], MULT)
+
+        def weave(t):
+            for c in range(NCH):
+                nc.scalar.copy(zq[c][:, :, t], z[t][:, c * CH : (c + 1) * CH])
+
+        gather(0)
+        gather(1)
+        scatter(0)
+        gather(2)
+        weave(0)
+        scatter(1)
+        gather(3)
+        weave(1)
+        scatter(2)
+        weave(2)
+        scatter(3)
+        weave(3)
+
+        ow = sb.tile([P, S], U32, name="ow", align_bytes=64)
+        osc = sb.tile([P, S], U8, name="osc", align_bytes=64)
+        out_rows = out_0.rearrange("(p t) j -> p t j", t=PACK)
+        accs = []
+        for c in range(NCH):
+            zc = sb.tile([P, CH], U32, name=f"zc{c}", align_bytes=64)
+            zs = sb.tile([P, CH], U8, name=f"zs{c}", align_bytes=64)
+            nc.vector.quantize_mx(out=zc[:].bitcast(FP8X4), scales=zs[:], in_=zq[c][:].rearrange("p n j -> p (n j)"))
+            acc = ps.tile([P, PACK, CH], F32, name=f"o_acc{c}")
+            for t in range(PACK):
+                nc.tensor.matmul_mx(
+                    out=acc[:, t, :], lhsT=w2wd[:, 2 * P * t : 2 * P * (t + 1)].bitcast(FP4X4), lhsT_scale=w2sd[:, P * t : P * (t + 1)],
+                    rhs=zc[:].bitcast(FP8X4), rhs_scale=zs[:], start=True, stop=True,
+                )
+            accs.append(acc)
+        for c in range(NCH):
+            cols = slice(c * CH, (c + 1) * CH)
+            o32 = sb.tile([P, PACK, CH], F32, name=f"o32_{c}", align_bytes=64)
+            if c == 0:
+                nc.vector.tensor_copy(o32[:], accs[c][:])
+            else:
+                nc.scalar.copy(o32[:], accs[c][:])
+            nc.sync.dma_start(out_rows[:, :, cols], o32[:])
+            oq = sb.tile([P, CH * PACK], BF16, name=f"oq{c}", align_bytes=64)
+            nc.vector.tensor_copy(
+                oq[:].rearrange("p (n i t) -> p n t i", i=4, t=PACK), o32[:].rearrange("p t (n i) -> p n t i", i=4)
+            )
+            nc.vector.quantize_mx(out=ow[:, cols].bitcast(FP8X4), scales=osc[:, cols], in_=oq[:])
+            if c % 2 == 1:
+                pair = slice((c - 1) * CH, (c + 1) * CH)
+                nc.sync.dma_start(out_1[0, :, pair, :].rearrange("p c r -> p (c r)").bitcast(I32), ow[:, pair].bitcast(I32))
+        for q in range(QUADS):
+            eng = nc.scalar if q % 2 else nc.sync
+            eng.dma_start(out_2[0, 4 * q : 4 * q + 4, :].bitcast(I32), osc[32 * q : 32 * q + 4, :].bitcast(I32))

@@ -23,6 +23,8 @@ QUADS = 4
 HALF = P // 2
 CH = 128
 NCH = S // CH
+ORDER = (2, 0, 1, 3)
+SPLIT = (0, 3)
 
 
 def tile_picked_modtrue_silu_po_kernel(
@@ -31,109 +33,119 @@ def tile_picked_modtrue_silu_po_kernel(
     nc = tc.nc
     with ExitStack() as ctx:
         sb = ctx.enter_context(tc.tile_pool(name="sb", bufs=1))
+        reuse = ctx.enter_context(tc.tile_pool(name="reuse", bufs=1))
         ps = ctx.enter_context(tc.psum_pool(name="ps", bufs=1))
 
         offs_t = sb.tile([P, S // 16], U16, name="offs_t")
         take_t = sb.tile([P, V // 16], U16, name="take_t")
-        xw = sb.tile([P, T], U32, name="xw", align_bytes=64)
+        xw = reuse.tile([P, T], U32, name="xw", align_bytes=64, offset=0)
         xs = sb.tile([P, T], U8, name="xs", align_bytes=64)
         w2w = sb.tile([P, 2 * N], U8, name="w2w", align_bytes=64)
         w2s = sb.tile([P, N], U8, name="w2s", align_bytes=64)
         gate = sb.tile([P, V], F32, name="gate", align_bytes=64)
         warm_in = sb.tile([P, 8], F32, name="warm_in")
         warm_out = sb.tile([P, 8], F32, name="warm_out")
-        w1raw = [sb.tile([P, PACK, H // 2], F32, name=f"w1raw{h}", align_bytes=64) for h in range(2)]
+        w1raw = [sb.tile([P, 2, H], F32, name=f"w1raw{a}", align_bytes=64) for a in range(2)]
 
         nc.vector.memset(xs[:].bitcast(I32), 0)
         nc.vector.memset(w2s[:].bitcast(I32), 0)
         nc.vector.memset(warm_in[:], 0.0)
 
         nc.sync.dma_start(offs_t[:], offs)
-        for q in range(QUADS):
-            nc.scalar.dma_start(xs[32 * q : 32 * q + 4, :].bitcast(I32), x_scales[0, 4 * q : 4 * q + 4, :].bitcast(I32))
-        nc.sync.dma_start(xw[:].bitcast(I32), x_words[0].rearrange("p c r -> p (c r)").bitcast(I32))
         w1_rows = w1.rearrange("(p j) c -> p j c", j=PACK)
-        for h in range(2):
-            nc.sync.dma_start(w1raw[h][:], w1_rows[:, :, h * (H // 2) : (h + 1) * (H // 2)])
+        nc.sync.dma_start(w1raw[0][:], w1_rows[:, 0:2, :])
+        for q in range(QUADS):
+            nc.sync.dma_start(xs[32 * q : 32 * q + 4, :].bitcast(I32), x_scales[0, 4 * q : 4 * q + 4, :].bitcast(I32))
+        nc.sync.dma_start(w1raw[1][:], w1_rows[:, 2:4, :])
+        nc.sync.dma_start(xw[:].bitcast(I32), x_words[0].rearrange("p c r -> p (c r)").bitcast(I32))
         nc.sync.dma_start(take_t[:], take)
-        nc.sync.dma_start(gate[:], wt.rearrange("(p j) v -> p j v", j=PACK)[:, 0, :])
         nc.sync.dma_start(w2w[:].bitcast(I32), w2_words[0].bitcast(I32))
         for q in range(QUADS):
             nc.sync.dma_start(w2s[32 * q : 32 * q + 4, :].bitcast(I32), w2_scales[0, 4 * q : 4 * q + 4, :].bitcast(I32))
+        nc.sync.dma_start(gate[:], wt.rearrange("(p j) v -> p j v", j=PACK)[:, 0, :])
 
         nc.scalar.activation(warm_out[:], warm_in[:], SILU)
 
         xsg = sb.tile([P, S], U8, name="xsg", align_bytes=64)
         xwg = sb.tile([P, S], U32, name="xwg", align_bytes=64)
         nc.vector.tensor_copy(xsg[:], xs[:].indirect(offs_t[:]))
-        nc.vector.tensor_copy(xwg[:], xw[:].indirect(offs_t[:]))
 
-        w1c = sb.tile([P, H], U32, name="w1c", align_bytes=64)
-        w1s = sb.tile([P, H], U8, name="w1s", align_bytes=64)
-        w1g = [sb.tile([P, PACK * HALF * PACK], BF16, name=f"w1g{h}", align_bytes=64) for h in range(2)]
+        w1c = [sb.tile([P, 2 * P], U32, name=f"w1c{e}", align_bytes=64) for e in range(2)]
+        w1s = [sb.tile([P, 2 * P], U8, name=f"w1s{e}", align_bytes=64) for e in range(2)]
+        w1g = [sb.tile([P, 2 * P * PACK], BF16, name=f"w1g{e}", align_bytes=64) for e in range(2)]
+        for a in range(2):
+            for e in range(2):
+                dst = w1g[e][:].rearrange("p (u m a j) -> p a m u j", u=2, a=2, j=2)[:, a]
+                src = w1raw[a][:].rearrange("p j (m u e) -> p e m u j", u=2, e=2)[:, e]
+                if (a, e) == (1, 0):
+                    nc.vector.tensor_copy(dst, src)
+                else:
+                    nc.scalar.copy(dst, src)
+        for e in range(2):
+            nc.vector.quantize_mx(out=w1c[e][:].bitcast(FP8X4), scales=w1s[e][:], in_=w1g[e][:])
+
         for h in range(2):
-            dst = w1g[h][:].rearrange("p (t m j) -> p m t j", t=PACK, j=PACK)
-            src = w1raw[h][:].rearrange("p j (m t) -> p m t j", t=PACK)
-            if h == 0:
-                nc.scalar.copy(dst, src)
-            else:
-                nc.vector.tensor_copy(dst, src)
-            for t in range(PACK):
-                cols = slice(P * t + HALF * h, P * t + HALF * (h + 1))
-                nc.vector.quantize_mx(
-                    out=w1c[:, cols].bitcast(FP8X4),
-                    scales=w1s[:, cols],
-                    in_=w1g[h][:, t * HALF * PACK : (t + 1) * HALF * PACK],
-                )
+            nc.vector.tensor_copy(xwg[:, h * 256 : (h + 1) * 256], xw[:].indirect(offs_t[:, 16 * h : 16 * (h + 1)]))
 
-        z = []
-        for t in range(PACK):
-            cols = slice(P * t, P * (t + 1))
-            acc = ps.tile([P, S], F32, name=f"y_acc{t}")
-            nc.tensor.matmul_mx(
-                out=acc[:], lhsT=w1c[:, cols].bitcast(FP8X4), lhsT_scale=w1s[:, cols],
-                rhs=xwg[:].bitcast(FP8X4), rhs_scale=xsg[:], start=True, stop=True,
-            )
-            zt = sb.tile([P, S], F32, name=f"z{t}", align_bytes=64)
-            nc.scalar.copy(zt[:], acc[:])
-            z.append(zt)
-
-        w2wd = sb.tile([P, 2 * N], U8, name="w2wd", align_bytes=64)
-        w2sd = sb.tile([P, N], U8, name="w2sd", align_bytes=64)
+        w2wd = reuse.tile([P, 2 * N], U8, name="w2wd", align_bytes=64, offset=0)
+        w2sd = reuse.tile([P, N], U8, name="w2sd", align_bytes=64, offset=2 * N)
         nc.vector.tensor_copy(
-            w2wd[:].rearrange("p (t m b) -> p m t b", t=PACK, b=2), w2w[:].rearrange("p (m t b) -> p m t b", t=PACK, b=2)
+            w2wd[:].rearrange("p (t m b) -> p t m b", t=PACK, b=2), w2w[:].rearrange("p (m t b) -> p t m b", t=PACK, b=2)
         )
-        nc.vector.tensor_copy(w2sd[:].rearrange("p (t m) -> p m t", t=PACK), w2s[:].rearrange("p (m t) -> p m t", t=PACK))
+        nc.vector.tensor_copy(w2sd[:].rearrange("p (t m) -> p t m", t=PACK), w2s[:].rearrange("p (m t) -> p t m", t=PACK))
+
+        z = {}
+
+        def layer1(t):
+            u, e = divmod(t, 2)
+            cols = slice(P * u, P * (u + 1))
+            zt = sb.tile([P, S], F32, name=f"z{t}", align_bytes=64, tag=f"z{t}")
+            pieces = 2 if t == ORDER[0] else 1
+            for h in range(pieces):
+                tok = slice(h * S // pieces, (h + 1) * S // pieces)
+                acc = ps.tile([P, S // pieces], F32, name=f"y_acc{t}_{h}", tag=f"bank{(t + 4 * h)}")
+                nc.tensor.matmul_mx(
+                    out=acc[:], lhsT=w1c[e][:, cols].bitcast(FP8X4), lhsT_scale=w1s[e][:, cols],
+                    rhs=xwg[:, tok].bitcast(FP8X4), rhs_scale=xsg[:, tok], start=True, stop=True,
+                )
+                nc.scalar.copy(zt[:, tok], acc[:])
+            z[t] = zt
 
         zq = [sb.tile([P, CH, PACK], BF16, name=f"zq{c}", align_bytes=64) for c in range(NCH)]
-        act = []
+        act = {}
 
         def gather(t):
             g = sb.tile([P, V], F32, name=f"g{t}", align_bytes=64)
             nc.vector.tensor_copy(g[:], z[t][:].indirect(take_t[:]))
-            a = sb.tile([P, V], F32, name=f"a{t}", align_bytes=64)
+            a = sb.tile([P, V], F32, name=f"a{t}", align_bytes=64, tag=f"z{ORDER[0]}" if t == ORDER[-1] else f"a{t}")
             nc.scalar.activation(a[:], g[:], SILU)
-            act.append(a)
+            act[t] = a
 
         def scatter(t):
             nc.vector.tensor_tensor(z[t][:].indirect(take_t[:]), act[t][:], gate[:], MULT)
 
         def weave(t):
             for c in range(NCH):
-                nc.scalar.copy(zq[c][:, :, t], z[t][:, c * CH : (c + 1) * CH])
+                if t == ORDER[-1] and c < NCH // 2:
+                    nc.vector.tensor_copy(zq[c][:, :, t], z[t][:, c * CH : (c + 1) * CH])
+                else:
+                    nc.scalar.copy(zq[c][:, :, t], z[t][:, c * CH : (c + 1) * CH])
 
-        gather(0)
-        gather(1)
-        scatter(0)
-        gather(2)
-        weave(0)
-        scatter(1)
-        gather(3)
-        weave(1)
-        scatter(2)
-        weave(2)
-        scatter(3)
-        weave(3)
+        first, second, third, last = ORDER
+        for t in ORDER:
+            layer1(t)
+        gather(first)
+        gather(second)
+        scatter(first)
+        weave(first)
+        gather(third)
+        scatter(second)
+        gather(last)
+        weave(second)
+        scatter(third)
+        weave(third)
+        scatter(last)
+        weave(last)
 
         ow = sb.tile([P, S], U32, name="ow", align_bytes=64)
         osc = sb.tile([P, S], U8, name="osc", align_bytes=64)
@@ -143,29 +155,35 @@ def tile_picked_modtrue_silu_po_kernel(
             zc = sb.tile([P, CH], U32, name=f"zc{c}", align_bytes=64)
             zs = sb.tile([P, CH], U8, name=f"zs{c}", align_bytes=64)
             nc.vector.quantize_mx(out=zc[:].bitcast(FP8X4), scales=zs[:], in_=zq[c][:].rearrange("p n j -> p (n j)"))
-            acc = ps.tile([P, PACK, CH], F32, name=f"o_acc{c}")
+            split = c in SPLIT
+            if split:
+                banks = [ps.tile([P, 2, CH], F32, name=f"o_acc{c}_{u}", tag=f"bank{c + 4 * u}") for u in range(2)]
+            else:
+                banks = [ps.tile([P, PACK, CH], F32, name=f"o_acc{c}", tag=f"bank{c}")]
             for t in range(PACK):
+                dst = banks[t // 2][:, t % 2, :] if split else banks[0][:, t, :]
                 nc.tensor.matmul_mx(
-                    out=acc[:, t, :], lhsT=w2wd[:, 2 * P * t : 2 * P * (t + 1)].bitcast(FP4X4), lhsT_scale=w2sd[:, P * t : P * (t + 1)],
+                    out=dst, lhsT=w2wd[:, 2 * P * t : 2 * P * (t + 1)].bitcast(FP4X4), lhsT_scale=w2sd[:, P * t : P * (t + 1)],
                     rhs=zc[:].bitcast(FP8X4), rhs_scale=zs[:], start=True, stop=True,
                 )
-            accs.append(acc)
+            accs.append(banks)
         for c in range(NCH):
             cols = slice(c * CH, (c + 1) * CH)
             o32 = sb.tile([P, PACK, CH], F32, name=f"o32_{c}", align_bytes=64)
-            if c == 0:
-                nc.vector.tensor_copy(o32[:], accs[c][:])
+            if c in SPLIT:
+                nc.vector.tensor_copy(o32[:, 0:2, :], accs[c][0][:])
+                nc.scalar.copy(o32[:, 2:4, :], accs[c][1][:])
             else:
-                nc.scalar.copy(o32[:], accs[c][:])
+                nc.scalar.copy(o32[:], accs[c][0][:])
             nc.sync.dma_start(out_rows[:, :, cols], o32[:])
             oq = sb.tile([P, CH * PACK], BF16, name=f"oq{c}", align_bytes=64)
             nc.vector.tensor_copy(
                 oq[:].rearrange("p (n i t) -> p n t i", i=4, t=PACK), o32[:].rearrange("p t (n i) -> p n t i", i=4)
             )
             nc.vector.quantize_mx(out=ow[:, cols].bitcast(FP8X4), scales=osc[:, cols], in_=oq[:])
-            if c % 2 == 1:
-                pair = slice((c - 1) * CH, (c + 1) * CH)
-                nc.sync.dma_start(out_1[0, :, pair, :].rearrange("p c r -> p (c r)").bitcast(I32), ow[:, pair].bitcast(I32))
+            if c >= NCH - 2:
+                done = slice(0 if c == NCH - 2 else c * CH, (c + 1) * CH)
+                nc.sync.dma_start(out_1[0, :, done, :].rearrange("p c r -> p (c r)").bitcast(I32), ow[:, done].bitcast(I32))
         for q in range(QUADS):
-            eng = nc.scalar if q % 2 else nc.sync
+            eng = nc.sync if q % 2 else nc.scalar
             eng.dma_start(out_2[0, 4 * q : 4 * q + 4, :].bitcast(I32), osc[32 * q : 32 * q + 4, :].bitcast(I32))

@@ -42,33 +42,36 @@ def tile_picked_modtrue_silu_po_kernel(
         xs = sb.tile([P, T], U8, name="xs", align_bytes=64)
         w2w = sb.tile([P, 2 * N], U8, name="w2w", align_bytes=64)
         w2s = sb.tile([P, N], U8, name="w2s", align_bytes=64)
-        gate = sb.tile([P, V], F32, name="gate", align_bytes=64)
+        xsp = sb.tile([P, S], U8, name="xsp", align_bytes=64)
         warm_in = sb.tile([P, 8], F32, name="warm_in")
         warm_out = sb.tile([P, 8], F32, name="warm_out")
+        w2sp = sb.tile([P, N], U8, name="w2sp", align_bytes=64)
+        gate = sb.tile([P, V], F32, name="gate", align_bytes=64)
         w1raw = [sb.tile([P, 2, H], F32, name=f"w1raw{a}", align_bytes=64) for a in range(2)]
 
         nc.vector.memset(xs[:].bitcast(I32), 0)
         nc.vector.memset(w2s[:].bitcast(I32), 0)
+        nc.vector.memset(xsp[:].bitcast(I32), 0)
+        nc.vector.memset(w2sp[:].bitcast(I32), 0)
         nc.vector.memset(warm_in[:], 0.0)
-
-        nc.sync.dma_start(offs_t[:], offs)
-        w1_rows = w1.rearrange("(p j) c -> p j c", j=PACK)
-        nc.sync.dma_start(w1raw[0][:], w1_rows[:, 0:2, :])
-        for q in range(QUADS):
-            nc.sync.dma_start(xs[32 * q : 32 * q + 4, :].bitcast(I32), x_scales[0, 4 * q : 4 * q + 4, :].bitcast(I32))
-        nc.sync.dma_start(w1raw[1][:], w1_rows[:, 2:4, :])
-        nc.sync.dma_start(xw[:].bitcast(I32), x_words[0].rearrange("p c r -> p (c r)").bitcast(I32))
-        nc.sync.dma_start(take_t[:], take)
-        nc.sync.dma_start(w2w[:].bitcast(I32), w2_words[0].bitcast(I32))
-        for q in range(QUADS):
-            nc.sync.dma_start(w2s[32 * q : 32 * q + 4, :].bitcast(I32), w2_scales[0, 4 * q : 4 * q + 4, :].bitcast(I32))
-        nc.sync.dma_start(gate[:], wt.rearrange("(p j) v -> p j v", j=PACK)[:, 0, :])
-
         nc.scalar.activation(warm_out[:], warm_in[:], SILU)
 
+        w1_rows = w1.rearrange("(p j) c -> p j c", j=PACK)
+        nc.sync.dma_start(w1raw[0][:], w1_rows[:, 0:2, :])
+        nc.sync.dma_start(offs_t[:], offs)
+        nc.sync.dma_start(xs[0:P:8, :].bitcast(I32), x_scales[0].bitcast(I32))
+        nc.sync.dma_start(w1raw[1][:], w1_rows[:, 2:4, :])
+        nc.sync.dma_start(xw[:].bitcast(I32), x_words[0].rearrange("p c r -> p (c r)").bitcast(I32))
         xsg = sb.tile([P, S], U8, name="xsg", align_bytes=64)
-        xwg = sb.tile([P, S], U32, name="xwg", align_bytes=64)
         nc.vector.tensor_copy(xsg[:], xs[:].indirect(offs_t[:]))
+        for q in range(QUADS):
+            nc.sync.dma_start(xsp[32 * q : 32 * q + 4, :].bitcast(I32), xsg[32 * q : 32 * q + 32 : 8, :].bitcast(I32))
+        nc.sync.dma_start(w2w[:].bitcast(I32), w2_words[0].bitcast(I32))
+        nc.sync.dma_start(w2s[0:P:8, :].bitcast(I32), w2_scales[0].bitcast(I32))
+        nc.sync.dma_start(take_t[:], take)
+        nc.sync.dma_start(gate[:], wt.rearrange("(p j) v -> p j v", j=PACK)[:, 0, :])
+
+        xwg = sb.tile([P, S], U32, name="xwg", align_bytes=64)
 
         w1c = [sb.tile([P, 2 * P], U32, name=f"w1c{e}", align_bytes=64) for e in range(2)]
         w1s = [sb.tile([P, 2 * P], U8, name=f"w1s{e}", align_bytes=64) for e in range(2)]
@@ -93,6 +96,8 @@ def tile_picked_modtrue_silu_po_kernel(
             w2wd[:].rearrange("p (t m b) -> p t m b", t=PACK, b=2), w2w[:].rearrange("p (m t b) -> p t m b", t=PACK, b=2)
         )
         nc.vector.tensor_copy(w2sd[:].rearrange("p (t m) -> p t m", t=PACK), w2s[:].rearrange("p (m t) -> p t m", t=PACK))
+        for q in range(QUADS):
+            nc.sync.dma_start(w2sp[32 * q : 32 * q + 4, :].bitcast(I32), w2sd[32 * q : 32 * q + 32 : 8, :].bitcast(I32))
 
         z = {}
 
@@ -106,7 +111,7 @@ def tile_picked_modtrue_silu_po_kernel(
                 acc = ps.tile([P, S // pieces], F32, name=f"y_acc{t}_{h}", tag=f"bank{(t + 4 * h)}")
                 nc.tensor.matmul_mx(
                     out=acc[:], lhsT=w1c[e][:, cols].bitcast(FP8X4), lhsT_scale=w1s[e][:, cols],
-                    rhs=xwg[:, tok].bitcast(FP8X4), rhs_scale=xsg[:, tok], start=True, stop=True,
+                    rhs=xwg[:, tok].bitcast(FP8X4), rhs_scale=xsp[:, tok], start=True, stop=True,
                 )
                 nc.scalar.copy(zt[:, tok], acc[:])
             z[t] = zt
@@ -126,7 +131,7 @@ def tile_picked_modtrue_silu_po_kernel(
 
         def weave(t):
             for c in range(NCH):
-                if t == ORDER[-1] and c < NCH // 2:
+                if t == ORDER[-1]:
                     nc.vector.tensor_copy(zq[c][:, :, t], z[t][:, c * CH : (c + 1) * CH])
                 else:
                     nc.scalar.copy(zq[c][:, :, t], z[t][:, c * CH : (c + 1) * CH])
@@ -163,14 +168,17 @@ def tile_picked_modtrue_silu_po_kernel(
             for t in range(PACK):
                 dst = banks[t // 2][:, t % 2, :] if split else banks[0][:, t, :]
                 nc.tensor.matmul_mx(
-                    out=dst, lhsT=w2wd[:, 2 * P * t : 2 * P * (t + 1)].bitcast(FP4X4), lhsT_scale=w2sd[:, P * t : P * (t + 1)],
+                    out=dst, lhsT=w2wd[:, 2 * P * t : 2 * P * (t + 1)].bitcast(FP4X4), lhsT_scale=w2sp[:, P * t : P * (t + 1)],
                     rhs=zc[:].bitcast(FP8X4), rhs_scale=zs[:], start=True, stop=True,
                 )
             accs.append(banks)
         for c in range(NCH):
             cols = slice(c * CH, (c + 1) * CH)
             o32 = sb.tile([P, PACK, CH], F32, name=f"o32_{c}", align_bytes=64)
-            if c in SPLIT:
+            if c == 0:
+                nc.scalar.copy(o32[:, 0:2, :], accs[c][0][:])
+                nc.scalar.copy(o32[:, 2:4, :], accs[c][1][:])
+            elif c == NCH - 1:
                 nc.vector.tensor_copy(o32[:, 0:2, :], accs[c][0][:])
                 nc.scalar.copy(o32[:, 2:4, :], accs[c][1][:])
             else:

@@ -24,7 +24,6 @@ HALF = P // 2
 CH = 128
 NCH = S // CH
 ORDER = (2, 0, 1, 3)
-SPLIT = (0, 3)
 
 
 def tile_picked_modtrue_silu_po_kernel(
@@ -61,14 +60,14 @@ def tile_picked_modtrue_silu_po_kernel(
         nc.sync.dma_start(offs_t[:], offs)
         nc.sync.dma_start(xs[0:P:8, :].bitcast(I32), x_scales[0].bitcast(I32))
         nc.sync.dma_start(w1raw[1][:], w1_rows[:, 2:4, :])
+        nc.sync.dma_start(w2s[0:P:8, :].bitcast(I32), w2_scales[0].bitcast(I32))
         nc.sync.dma_start(xw[:].bitcast(I32), x_words[0].rearrange("p c r -> p (c r)").bitcast(I32))
         xsg = sb.tile([P, S], U8, name="xsg", align_bytes=64)
         nc.vector.tensor_copy(xsg[:], xs[:].indirect(offs_t[:]))
         for q in range(QUADS):
             nc.sync.dma_start(xsp[32 * q : 32 * q + 4, :].bitcast(I32), xsg[32 * q : 32 * q + 32 : 8, :].bitcast(I32))
-        nc.sync.dma_start(w2w[:].bitcast(I32), w2_words[0].bitcast(I32))
-        nc.sync.dma_start(w2s[0:P:8, :].bitcast(I32), w2_scales[0].bitcast(I32))
         nc.sync.dma_start(take_t[:], take)
+        nc.sync.dma_start(w2w[:].bitcast(I32), w2_words[0].bitcast(I32))
         nc.sync.dma_start(gate[:], wt.rearrange("(p j) v -> p j v", j=PACK)[:, 0, :])
 
         xwg = sb.tile([P, S], U32, name="xwg", align_bytes=64)
@@ -91,7 +90,7 @@ def tile_picked_modtrue_silu_po_kernel(
             nc.vector.tensor_copy(xwg[:, h * 256 : (h + 1) * 256], xw[:].indirect(offs_t[:, 16 * h : 16 * (h + 1)]))
 
         w2wd = reuse.tile([P, 2 * N], U8, name="w2wd", align_bytes=64, offset=0)
-        w2sd = reuse.tile([P, N], U8, name="w2sd", align_bytes=64, offset=2 * N)
+        w2sd = sb.tile([P, N], U8, name="w2sd", align_bytes=64)
         nc.vector.tensor_copy(
             w2wd[:].rearrange("p (t m b) -> p t m b", t=PACK, b=2), w2w[:].rearrange("p (m t b) -> p t m b", t=PACK, b=2)
         )
@@ -99,22 +98,17 @@ def tile_picked_modtrue_silu_po_kernel(
         for q in range(QUADS):
             nc.sync.dma_start(w2sp[32 * q : 32 * q + 4, :].bitcast(I32), w2sd[32 * q : 32 * q + 32 : 8, :].bitcast(I32))
 
-        z = {}
+        z = {t: sb.tile([P, S], F32, name=f"z{t}", align_bytes=64, tag=f"z{t}") for t in ORDER}
 
-        def layer1(t):
+        def layer1(t, tok, bank):
             u, e = divmod(t, 2)
             cols = slice(P * u, P * (u + 1))
-            zt = sb.tile([P, S], F32, name=f"z{t}", align_bytes=64, tag=f"z{t}")
-            pieces = 2 if t == ORDER[0] else 1
-            for h in range(pieces):
-                tok = slice(h * S // pieces, (h + 1) * S // pieces)
-                acc = ps.tile([P, S // pieces], F32, name=f"y_acc{t}_{h}", tag=f"bank{(t + 4 * h)}")
-                nc.tensor.matmul_mx(
-                    out=acc[:], lhsT=w1c[e][:, cols].bitcast(FP8X4), lhsT_scale=w1s[e][:, cols],
-                    rhs=xwg[:, tok].bitcast(FP8X4), rhs_scale=xsp[:, tok], start=True, stop=True,
-                )
-                nc.scalar.copy(zt[:, tok], acc[:])
-            z[t] = zt
+            acc = ps.tile([P, tok.stop - tok.start], F32, name=f"y_acc{bank}", tag=f"bank{bank}")
+            nc.tensor.matmul_mx(
+                out=acc[:], lhsT=w1c[e][:, cols].bitcast(FP8X4), lhsT_scale=w1s[e][:, cols],
+                rhs=xwg[:, tok].bitcast(FP8X4), rhs_scale=xsp[:, tok], start=True, stop=True,
+            )
+            nc.scalar.copy(z[t][:, tok], acc[:])
 
         zq = [sb.tile([P, CH, PACK], BF16, name=f"zq{c}", align_bytes=64) for c in range(NCH)]
         act = {}
@@ -131,14 +125,15 @@ def tile_picked_modtrue_silu_po_kernel(
 
         def weave(t):
             for c in range(NCH):
-                if t == ORDER[-1]:
-                    nc.vector.tensor_copy(zq[c][:, :, t], z[t][:, c * CH : (c + 1) * CH])
-                else:
-                    nc.scalar.copy(zq[c][:, :, t], z[t][:, c * CH : (c + 1) * CH])
+                nc.scalar.copy(zq[c][:, :, t], z[t][:, c * CH : (c + 1) * CH])
 
         first, second, third, last = ORDER
-        for t in ORDER:
-            layer1(t)
+        for h in range(2):
+            tok = slice(h * S // 2, (h + 1) * S // 2)
+            layer1(first, tok, 2 * h)
+            layer1(second, tok, 2 * h + 1)
+        layer1(third, slice(0, S), 4)
+        layer1(last, slice(0, S), 5)
         gather(first)
         gather(second)
         scatter(first)
@@ -150,48 +145,59 @@ def tile_picked_modtrue_silu_po_kernel(
         scatter(third)
         weave(third)
         scatter(last)
-        weave(last)
+
+        zc = [sb.tile([P, CH], U32, name=f"zc{c}", align_bytes=64) for c in range(NCH)]
+        zs = [sb.tile([P, CH], U8, name=f"zs{c}", align_bytes=64) for c in range(NCH)]
+
+        def quantise_z(c):
+            nc.vector.quantize_mx(out=zc[c][:].bitcast(FP8X4), scales=zs[c][:], in_=zq[c][:].rearrange("p n j -> p (n j)"))
+
+        for c in range(NCH):
+            nc.vector.tensor_copy(zq[c][:, :, last], z[last][:, c * CH : (c + 1) * CH])
+            if c > 0:
+                quantise_z(c - 1)
+        quantise_z(NCH - 1)
 
         ow = sb.tile([P, S], U32, name="ow", align_bytes=64)
         osc = sb.tile([P, S], U8, name="osc", align_bytes=64)
         out_rows = out_0.rearrange("(p t) j -> p t j", t=PACK)
-        accs = []
+        o32 = [sb.tile([P, PACK, CH], F32, name=f"o32_{c}", align_bytes=64) for c in range(NCH)]
         for c in range(NCH):
-            zc = sb.tile([P, CH], U32, name=f"zc{c}", align_bytes=64)
-            zs = sb.tile([P, CH], U8, name=f"zs{c}", align_bytes=64)
-            nc.vector.quantize_mx(out=zc[:].bitcast(FP8X4), scales=zs[:], in_=zq[c][:].rearrange("p n j -> p (n j)"))
-            split = c in SPLIT
-            if split:
-                banks = [ps.tile([P, 2, CH], F32, name=f"o_acc{c}_{u}", tag=f"bank{c + 4 * u}") for u in range(2)]
-            else:
-                banks = [ps.tile([P, PACK, CH], F32, name=f"o_acc{c}", tag=f"bank{c}")]
-            for t in range(PACK):
-                dst = banks[t // 2][:, t % 2, :] if split else banks[0][:, t, :]
-                nc.tensor.matmul_mx(
-                    out=dst, lhsT=w2wd[:, 2 * P * t : 2 * P * (t + 1)].bitcast(FP4X4), lhsT_scale=w2sp[:, P * t : P * (t + 1)],
-                    rhs=zc[:].bitcast(FP8X4), rhs_scale=zs[:], start=True, stop=True,
-                )
-            accs.append(banks)
-        for c in range(NCH):
-            cols = slice(c * CH, (c + 1) * CH)
-            o32 = sb.tile([P, PACK, CH], F32, name=f"o32_{c}", align_bytes=64)
-            if c == 0:
-                nc.scalar.copy(o32[:, 0:2, :], accs[c][0][:])
-                nc.scalar.copy(o32[:, 2:4, :], accs[c][1][:])
-            elif c == NCH - 1:
-                nc.vector.tensor_copy(o32[:, 0:2, :], accs[c][0][:])
-                nc.scalar.copy(o32[:, 2:4, :], accs[c][1][:])
-            else:
-                nc.scalar.copy(o32[:], accs[c][0][:])
-            nc.sync.dma_start(out_rows[:, :, cols], o32[:])
-            oq = sb.tile([P, CH * PACK], BF16, name=f"oq{c}", align_bytes=64)
+            for u in range(2):
+                bank = ps.tile([P, 2, CH], F32, name=f"o_acc{c}_{u}", tag=f"bank{2 * c + u}")
+                for i in range(2):
+                    t = 2 * u + i
+                    nc.tensor.matmul_mx(
+                        out=bank[:, i, :], lhsT=w2wd[:, 2 * P * t : 2 * P * (t + 1)].bitcast(FP4X4),
+                        lhsT_scale=w2sp[:, P * t : P * (t + 1)],
+                        rhs=zc[c][:].bitcast(FP8X4), rhs_scale=zs[c][:], start=True, stop=True,
+                    )
+                nc.scalar.copy(o32[c][:, 2 * u : 2 * u + 2, :], bank[:])
+            nc.sync.dma_start(out_rows[:, :, c * CH : (c + 1) * CH], o32[c][:])
+
+        def regroup(c, lo, hi):
+            oq = sb.tile([P, (hi - lo) * PACK], BF16, name=f"oq{c}_{lo}", align_bytes=64)
             nc.vector.tensor_copy(
-                oq[:].rearrange("p (n i t) -> p n t i", i=4, t=PACK), o32[:].rearrange("p t (n i) -> p n t i", i=4)
+                oq[:].rearrange("p (n i t) -> p n t i", i=4, t=PACK),
+                o32[c][:, :, lo:hi].rearrange("p t (n i) -> p n t i", i=4),
             )
+            return oq
+
+        def quantise_out(c, lo, hi, oq):
+            cols = slice(c * CH + lo, c * CH + hi)
             nc.vector.quantize_mx(out=ow[:, cols].bitcast(FP8X4), scales=osc[:, cols], in_=oq[:])
-            if c >= NCH - 2:
-                done = slice(0 if c == NCH - 2 else c * CH, (c + 1) * CH)
-                nc.sync.dma_start(out_1[0, :, done, :].rearrange("p c r -> p (c r)").bitcast(I32), ow[:, done].bitcast(I32))
+
+        def store_words(cols):
+            nc.sync.dma_start(out_1[0, :, cols, :].rearrange("p c r -> p (c r)").bitcast(I32), ow[:, cols].bitcast(I32))
+
+        for c in range(NCH - 1):
+            quantise_out(c, 0, CH, regroup(c, 0, CH))
+        store_words(slice(0, S - CH))
+        halves = [(0, CH // 2), (CH // 2, CH)]
+        grouped = [regroup(NCH - 1, lo, hi) for lo, hi in halves]
+        for (lo, hi), oq in zip(halves, grouped):
+            quantise_out(NCH - 1, lo, hi, oq)
+        store_words(slice(S - CH, S))
         for q in range(QUADS):
             eng = nc.sync if q % 2 else nc.scalar
             eng.dma_start(out_2[0, 4 * q : 4 * q + 4, :].bitcast(I32), osc[32 * q : 32 * q + 4, :].bitcast(I32))

@@ -153,10 +153,13 @@ def tile_picked_modtrue_silu_po_kernel(
             nc.vector.quantize_mx(out=zc[c][:].bitcast(FP8X4), scales=zs[c][:], in_=zq[c][:].rearrange("p n j -> p (n j)"))
 
         for c in range(NCH):
-            nc.vector.tensor_copy(zq[c][:, :, last], z[last][:, c * CH : (c + 1) * CH])
-            if c > 0:
-                quantise_z(c - 1)
-        quantise_z(NCH - 1)
+            dst, src = zq[c][:, :, last], z[last][:, c * CH : (c + 1) * CH]
+            if c < NCH // 2:
+                nc.vector.tensor_copy(dst, src)
+            else:
+                nc.scalar.copy(dst, src)
+        for c in range(NCH):
+            quantise_z(c)
 
         ow = sb.tile([P, S], U32, name="ow", align_bytes=64)
         osc = sb.tile([P, S], U8, name="osc", align_bytes=64)
@@ -173,7 +176,10 @@ def tile_picked_modtrue_silu_po_kernel(
                         rhs=zc[c][:].bitcast(FP8X4), rhs_scale=zs[c][:], start=True, stop=True,
                     )
                 nc.scalar.copy(o32[c][:, 2 * u : 2 * u + 2, :], bank[:])
-            nc.sync.dma_start(out_rows[:, :, c * CH : (c + 1) * CH], o32[c][:])
+                if c == 0:
+                    nc.sync.dma_start(out_rows[:, 2 * u : 2 * u + 2, 0:CH], o32[c][:, 2 * u : 2 * u + 2, :])
+            if c > 0:
+                nc.sync.dma_start(out_rows[:, :, c * CH : (c + 1) * CH], o32[c][:])
 
         def regroup(c, lo, hi):
             oq = sb.tile([P, (hi - lo) * PACK], BF16, name=f"oq{c}_{lo}", align_bytes=64)

@@ -98,7 +98,7 @@ def tile_picked_modtrue_silu_po_kernel(
         for q in range(QUADS):
             nc.sync.dma_start(w2sp[32 * q : 32 * q + 4, :].bitcast(I32), w2sd[32 * q : 32 * q + 32 : 8, :].bitcast(I32))
 
-        z = {t: sb.tile([P, S], F32, name=f"z{t}", align_bytes=64, tag=f"z{t}") for t in ORDER}
+        z = {t: sb.tile([P, S], F32, name=f"z{t}", align_bytes=64, tag=f"z{t}") for t in ORDER[:3]}
 
         def layer1(t, tok, bank):
             u, e = divmod(t, 2)
@@ -110,11 +110,14 @@ def tile_picked_modtrue_silu_po_kernel(
             )
             nc.scalar.copy(z[t][:, tok], acc[:])
 
-        zq = [sb.tile([P, CH, PACK], BF16, name=f"zq{c}", align_bytes=64) for c in range(NCH)]
+        zq = [sb.tile([P, 2 * CH, PACK], BF16, name=f"zq{h}", align_bytes=64) for h in range(2)]
         act = {}
 
         def gather(t):
-            g = sb.tile([P, V], F32, name=f"g{t}", align_bytes=64)
+            if t == ORDER[0]:
+                g = reuse.tile([P, V], F32, name=f"g{t}", align_bytes=64, offset=4 * T)
+            else:
+                g = sb.tile([P, V], F32, name=f"g{t}", align_bytes=64)
             nc.vector.tensor_copy(g[:], z[t][:].indirect(take_t[:]))
             a = sb.tile([P, V], F32, name=f"a{t}", align_bytes=64, tag=f"z{ORDER[0]}" if t == ORDER[-1] else f"a{t}")
             nc.scalar.activation(a[:], g[:], SILU)
@@ -124,8 +127,8 @@ def tile_picked_modtrue_silu_po_kernel(
             nc.vector.tensor_tensor(z[t][:].indirect(take_t[:]), act[t][:], gate[:], MULT)
 
         def weave(t):
-            for c in range(NCH):
-                nc.scalar.copy(zq[c][:, :, t], z[t][:, c * CH : (c + 1) * CH])
+            for h in range(2):
+                nc.scalar.copy(zq[h][:, :, t], z[t][:, 2 * CH * h : 2 * CH * (h + 1)])
 
         first, second, third, last = ORDER
         for h in range(2):
@@ -133,14 +136,15 @@ def tile_picked_modtrue_silu_po_kernel(
             layer1(first, tok, 2 * h)
             layer1(second, tok, 2 * h + 1)
         layer1(third, slice(0, S), 4)
-        layer1(last, slice(0, S), 5)
         gather(first)
+        z[last] = reuse.tile([P, S], F32, name="z_last", align_bytes=64, offset=4 * T)
+        layer1(last, slice(0, S), 5)
         gather(second)
+        gather(third)
         scatter(first)
         weave(first)
-        gather(third)
-        scatter(second)
         gather(last)
+        scatter(second)
         weave(second)
         scatter(third)
         weave(third)
@@ -150,14 +154,11 @@ def tile_picked_modtrue_silu_po_kernel(
         zs = [sb.tile([P, CH], U8, name=f"zs{c}", align_bytes=64) for c in range(NCH)]
 
         def quantise_z(c):
-            nc.vector.quantize_mx(out=zc[c][:].bitcast(FP8X4), scales=zs[c][:], in_=zq[c][:].rearrange("p n j -> p (n j)"))
+            nc.vector.quantize_mx(out=zc[c][:].bitcast(FP8X4), scales=zs[c][:], in_=zq[c // 2][:, (c % 2) * CH : (c % 2 + 1) * CH, :].rearrange("p n j -> p (n j)"))
 
-        for c in range(NCH):
-            dst, src = zq[c][:, :, last], z[last][:, c * CH : (c + 1) * CH]
-            if c < NCH // 2:
-                nc.vector.tensor_copy(dst, src)
-            else:
-                nc.scalar.copy(dst, src)
+        for c in range(2):
+            nc.vector.tensor_copy(zq[0][:, c * CH : (c + 1) * CH, last], z[last][:, c * CH : (c + 1) * CH])
+        nc.scalar.copy(zq[1][:, :, last], z[last][:, 2 * CH : S])
         for c in range(NCH):
             quantise_z(c)
 

@@ -23,6 +23,7 @@ QUADS = 4
 HALF = P // 2
 CH = 128
 NCH = S // CH
+SPANS = ((0, CH), (CH, 2 * CH), (2 * CH, S))
 ORDER = (2, 0, 1, 3)
 
 
@@ -150,61 +151,63 @@ def tile_picked_modtrue_silu_po_kernel(
         weave(third)
         scatter(last)
 
-        zc = [sb.tile([P, CH], U32, name=f"zc{c}", align_bytes=64) for c in range(NCH)]
-        zs = [sb.tile([P, CH], U8, name=f"zs{c}", align_bytes=64) for c in range(NCH)]
-
-        def quantise_z(c):
-            nc.vector.quantize_mx(out=zc[c][:].bitcast(FP8X4), scales=zs[c][:], in_=zq[c // 2][:, (c % 2) * CH : (c % 2 + 1) * CH, :].rearrange("p n j -> p (n j)"))
-
+        zc = [sb.tile([P, hi - lo], U32, name=f"zc{lo}", align_bytes=64) for lo, hi in SPANS]
+        zs = [sb.tile([P, hi - lo], U8, name=f"zs{lo}", align_bytes=64) for lo, hi in SPANS]
         for c in range(2):
             nc.vector.tensor_copy(zq[0][:, c * CH : (c + 1) * CH, last], z[last][:, c * CH : (c + 1) * CH])
         nc.scalar.copy(zq[1][:, :, last], z[last][:, 2 * CH : S])
-        for c in range(NCH):
-            quantise_z(c)
+        for c in range(2):
+            src = zq[0][:, c * CH : (c + 1) * CH, :]
+            nc.vector.quantize_mx(out=zc[c][:].bitcast(FP8X4), scales=zs[c][:], in_=src.rearrange("p n j -> p (n j)"))
+        nc.vector.quantize_mx(out=zc[2][:].bitcast(FP8X4), scales=zs[2][:], in_=zq[1][:].rearrange("p n j -> p (n j)"))
 
         ow = sb.tile([P, S], U32, name="ow", align_bytes=64)
         osc = sb.tile([P, S], U8, name="osc", align_bytes=64)
         out_rows = out_0.rearrange("(p t) j -> p t j", t=PACK)
-        o32 = [sb.tile([P, PACK, CH], F32, name=f"o32_{c}", align_bytes=64) for c in range(NCH)]
-        for c in range(NCH):
-            for u in range(2):
-                bank = ps.tile([P, 2, CH], F32, name=f"o_acc{c}_{u}", tag=f"bank{2 * c + u}")
-                for i in range(2):
-                    t = 2 * u + i
+        o32 = [sb.tile([P, PACK, hi - lo], F32, name=f"o32_{lo}", align_bytes=64) for lo, hi in SPANS]
+        nbank = 0
+        for c, (lo, hi) in enumerate(SPANS):
+            per = 2 * CH // (hi - lo)
+            for t0 in range(0, PACK, per):
+                bank = ps.tile([P, per, hi - lo], F32, name=f"o_acc{nbank}", tag=f"bank{nbank}")
+                nbank += 1
+                for i in range(per):
+                    t = t0 + i
                     nc.tensor.matmul_mx(
                         out=bank[:, i, :], lhsT=w2wd[:, 2 * P * t : 2 * P * (t + 1)].bitcast(FP4X4),
                         lhsT_scale=w2sp[:, P * t : P * (t + 1)],
                         rhs=zc[c][:].bitcast(FP8X4), rhs_scale=zs[c][:], start=True, stop=True,
                     )
-                nc.scalar.copy(o32[c][:, 2 * u : 2 * u + 2, :], bank[:])
-                if c == 0:
-                    nc.sync.dma_start(out_rows[:, 2 * u : 2 * u + 2, 0:CH], o32[c][:, 2 * u : 2 * u + 2, :])
-            if c > 0:
-                nc.sync.dma_start(out_rows[:, :, c * CH : (c + 1) * CH], o32[c][:])
+                nc.scalar.copy(o32[c][:, t0 : t0 + per, :], bank[:])
+                done = t0 + per
+                group = PACK if c == 1 else 2
+                if done % group == 0:
+                    nc.sync.dma_start(out_rows[:, done - group : done, lo:hi], o32[c][:, done - group : done, :])
 
-        def regroup(c, lo, hi):
-            oq = sb.tile([P, (hi - lo) * PACK], BF16, name=f"oq{c}_{lo}", align_bytes=64)
+        def regroup(dst, c, part, ts):
             nc.vector.tensor_copy(
-                oq[:].rearrange("p (n i t) -> p n t i", i=4, t=PACK),
-                o32[c][:, :, lo:hi].rearrange("p t (n i) -> p n t i", i=4),
+                dst[:].rearrange("p (n i t) -> p n t i", i=4, t=PACK)[:, :, ts],
+                o32[c][:, ts, part * CH : (part + 1) * CH].rearrange("p t (n i) -> p n t i", i=4),
             )
-            return oq
 
-        def quantise_out(c, lo, hi, oq):
-            cols = slice(c * CH + lo, c * CH + hi)
-            nc.vector.quantize_mx(out=ow[:, cols].bitcast(FP8X4), scales=osc[:, cols], in_=oq[:])
+        def quantise_out(k):
+            cols = slice(k * CH, (k + 1) * CH)
+            nc.vector.quantize_mx(out=ow[:, cols].bitcast(FP8X4), scales=osc[:, cols], in_=oq[k][:])
 
         def store_words(cols):
             nc.sync.dma_start(out_1[0, :, cols, :].rearrange("p c r -> p (c r)").bitcast(I32), ow[:, cols].bitcast(I32))
 
-        for c in range(NCH - 1):
-            quantise_out(c, 0, CH, regroup(c, 0, CH))
-        store_words(slice(0, S - CH))
-        halves = [(0, CH // 2), (CH // 2, CH)]
-        grouped = [regroup(NCH - 1, lo, hi) for lo, hi in halves]
-        for (lo, hi), oq in zip(halves, grouped):
-            quantise_out(NCH - 1, lo, hi, oq)
-        store_words(slice(S - CH, S))
+        oq = [sb.tile([P, CH * PACK], BF16, name=f"oq{k}", align_bytes=64) for k in range(NCH)]
+        for c in range(2):
+            regroup(oq[c], c, 0, slice(0, PACK))
+            quantise_out(c)
+        store_words(slice(0, 2 * CH))
+        for ts in (slice(0, 2), slice(2, PACK)):
+            for part in range(2):
+                regroup(oq[2 + part], 2, part, ts)
+        for part in range(2):
+            quantise_out(2 + part)
+        store_words(slice(2 * CH, S))
         for q in range(QUADS):
             eng = nc.sync if q % 2 else nc.scalar
             eng.dma_start(out_2[0, 4 * q : 4 * q + 4, :].bitcast(I32), osc[32 * q : 32 * q + 4, :].bitcast(I32))

@@ -20,11 +20,11 @@ MULT = mybir.AluOpType.mult
 P = 128
 PACK = 4
 QUADS = 4
-HALF = P // 2
 CH = 128
 NCH = S // CH
 SPANS = ((0, CH), (CH, 2 * CH), (2 * CH, S))
 ORDER = (2, 0, 1, 3)
+X_HEAD = T // 4
 
 
 def tile_picked_modtrue_silu_po_kernel(
@@ -34,19 +34,19 @@ def tile_picked_modtrue_silu_po_kernel(
     with ExitStack() as ctx:
         sb = ctx.enter_context(tc.tile_pool(name="sb", bufs=1))
         reuse = ctx.enter_context(tc.tile_pool(name="reuse", bufs=1))
+        late = ctx.enter_context(tc.tile_pool(name="late", bufs=1))
         ps = ctx.enter_context(tc.psum_pool(name="ps", bufs=1))
+        first, second, third, last = ORDER
 
         offs_t = sb.tile([P, S // 16], U16, name="offs_t")
         take_t = sb.tile([P, V // 16], U16, name="take_t")
-        xw = reuse.tile([P, T], U32, name="xw", align_bytes=64, offset=0)
-        xs = sb.tile([P, T], U8, name="xs", align_bytes=64)
-        w2w = sb.tile([P, 2 * N], U8, name="w2w", align_bytes=64)
+        xw = sb.tile([P, T], U32, name="xw", align_bytes=64)
+        xs = late.tile([P, T], U8, name="xs", align_bytes=64, offset=0)
         w2s = sb.tile([P, N], U8, name="w2s", align_bytes=64)
         xsp = sb.tile([P, S], U8, name="xsp", align_bytes=64)
+        w2sp = sb.tile([P, N], U8, name="w2sp", align_bytes=64)
         warm_in = sb.tile([P, 8], F32, name="warm_in")
         warm_out = sb.tile([P, 8], F32, name="warm_out")
-        w2sp = sb.tile([P, N], U8, name="w2sp", align_bytes=64)
-        gate = sb.tile([P, V], F32, name="gate", align_bytes=64)
         w1raw = [sb.tile([P, 2, H], F32, name=f"w1raw{a}", align_bytes=64) for a in range(2)]
 
         nc.vector.memset(xs[:].bitcast(I32), 0)
@@ -56,48 +56,68 @@ def tile_picked_modtrue_silu_po_kernel(
         nc.vector.memset(warm_in[:], 0.0)
         nc.scalar.activation(warm_out[:], warm_in[:], SILU)
 
+        x_rows = x_words[0].rearrange("p c r -> p (c r)").bitcast(I32)
         w1_rows = w1.rearrange("(p j) c -> p j c", j=PACK)
-        nc.sync.dma_start(w1raw[0][:], w1_rows[:, 0:2, :])
+        nc.sync.dma_start(xw[:, :X_HEAD].bitcast(I32), x_rows[:, :X_HEAD])
         nc.sync.dma_start(offs_t[:], offs)
         nc.sync.dma_start(xs[0:P:8, :].bitcast(I32), x_scales[0].bitcast(I32))
-        nc.sync.dma_start(w1raw[1][:], w1_rows[:, 2:4, :])
         nc.sync.dma_start(w2s[0:P:8, :].bitcast(I32), w2_scales[0].bitcast(I32))
-        nc.sync.dma_start(xw[:].bitcast(I32), x_words[0].rearrange("p c r -> p (c r)").bitcast(I32))
+        nc.sync.dma_start(xw[:, X_HEAD:].bitcast(I32), x_rows[:, X_HEAD:])
+        nc.sync.dma_start(w1raw[0][:], w1_rows[:, 0:2, :])
+        for j in range(2):
+            nc.sync.dma_start(w1raw[1][:, j, :], w1_rows[:, 2 + j, :])
+
         xsg = sb.tile([P, S], U8, name="xsg", align_bytes=64)
         nc.vector.tensor_copy(xsg[:], xs[:].indirect(offs_t[:]))
         for q in range(QUADS):
-            nc.sync.dma_start(xsp[32 * q : 32 * q + 4, :].bitcast(I32), xsg[32 * q : 32 * q + 32 : 8, :].bitcast(I32))
+            nc.scalar.dma_start(xsp[32 * q : 32 * q + 4, :].bitcast(I32), xsg[32 * q : 32 * q + 32 : 8, :].bitcast(I32))
         nc.sync.dma_start(take_t[:], take)
+        w2w = late.tile([P, 2 * N], U8, name="w2w", align_bytes=64, offset=0)
+        gate = late.tile([P, V], F32, name="gate", align_bytes=64, offset=2 * N)
         nc.sync.dma_start(w2w[:].bitcast(I32), w2_words[0].bitcast(I32))
         nc.sync.dma_start(gate[:], wt.rearrange("(p j) v -> p j v", j=PACK)[:, 0, :])
 
-        xwg = sb.tile([P, S], U32, name="xwg", align_bytes=64)
-
-        w1c = [sb.tile([P, 2 * P], U32, name=f"w1c{e}", align_bytes=64) for e in range(2)]
-        w1s = [sb.tile([P, 2 * P], U8, name=f"w1s{e}", align_bytes=64) for e in range(2)]
-        w1g = [sb.tile([P, 2 * P * PACK], BF16, name=f"w1g{e}", align_bytes=64) for e in range(2)]
-        for a in range(2):
-            for e in range(2):
-                dst = w1g[e][:].rearrange("p (u m a j) -> p a m u j", u=2, a=2, j=2)[:, a]
-                src = w1raw[a][:].rearrange("p j (m u e) -> p e m u j", u=2, e=2)[:, e]
-                if (a, e) == (1, 0):
-                    nc.vector.tensor_copy(dst, src)
-                else:
-                    nc.scalar.copy(dst, src)
-        for e in range(2):
-            nc.vector.quantize_mx(out=w1c[e][:].bitcast(FP8X4), scales=w1s[e][:], in_=w1g[e][:])
-
-        for h in range(2):
-            nc.vector.tensor_copy(xwg[:, h * 256 : (h + 1) * 256], xw[:].indirect(offs_t[:, 16 * h : 16 * (h + 1)]))
-
-        w2wd = reuse.tile([P, 2 * N], U8, name="w2wd", align_bytes=64, offset=0)
         w2sd = sb.tile([P, N], U8, name="w2sd", align_bytes=64)
-        nc.vector.tensor_copy(
-            w2wd[:].rearrange("p (t m b) -> p t m b", t=PACK, b=2), w2w[:].rearrange("p (m t b) -> p t m b", t=PACK, b=2)
-        )
         nc.vector.tensor_copy(w2sd[:].rearrange("p (t m) -> p t m", t=PACK), w2s[:].rearrange("p (m t) -> p t m", t=PACK))
         for q in range(QUADS):
             nc.sync.dma_start(w2sp[32 * q : 32 * q + 4, :].bitcast(I32), w2sd[32 * q : 32 * q + 32 : 8, :].bitcast(I32))
+
+        xwg = sb.tile([P, S], U32, name="xwg", align_bytes=64)
+        nc.vector.tensor_copy(xwg[:], xw[:].indirect(offs_t[:]))
+
+        w1c = [sb.tile([P, 2 * P], U32, name=f"w1c{e}", align_bytes=64) for e in range(2)]
+        w1s = [sb.tile([P, 2 * P], U8, name=f"w1s{e}", align_bytes=64) for e in range(2)]
+        w1g = [reuse.tile([P, 2 * P * PACK], BF16, name="w1g0", align_bytes=64, offset=0),
+               sb.tile([P, 2 * P * PACK], BF16, name="w1g1", align_bytes=64)]
+
+        def cast_views(a, e):
+            dst = w1g[e][:].rearrange("p (u m a j) -> p a u m j", u=2, a=2, j=2)[:, a]
+            src = w1raw[a][:].rearrange("p j (m u e) -> p e u m j", u=2, e=2)[:, e]
+            return dst, src
+
+        def cast_pair(eng, a, e):
+            dst, src = cast_views(a, e)
+            eng(dst.rearrange("p u m j -> p m u j"), src.rearrange("p u m j -> p m u j"))
+
+        cast_pair(nc.vector.tensor_copy, 0, 0)
+        cast_pair(nc.scalar.copy, 0, 1)
+        cast_pair(nc.scalar.copy, 1, 1)
+        dst, src = cast_views(1, 0)
+        nc.vector.tensor_copy(dst[:, :, :, 0].rearrange("p u m -> p m u"), src[:, :, :, 0].rearrange("p u m -> p m u"))
+        for t in (first, second):
+            nc.vector.tensor_copy(dst[:, t // 2, :, 1], src[:, t // 2, :, 1])
+        for t in (first, second):
+            u = t // 2
+            nc.vector.quantize_mx(
+                out=w1c[0][:, P * u : P * (u + 1)].bitcast(FP8X4), scales=w1s[0][:, P * u : P * (u + 1)],
+                in_=w1g[0][:, PACK * P * u : PACK * P * (u + 1)],
+            )
+        nc.vector.quantize_mx(out=w1c[1][:].bitcast(FP8X4), scales=w1s[1][:], in_=w1g[1][:])
+
+        w2wd = reuse.tile([P, 2 * N], U8, name="w2wd", align_bytes=64, offset=0)
+        nc.vector.tensor_copy(
+            w2wd[:].rearrange("p (t m b) -> p t m b", t=PACK, b=2), w2w[:].rearrange("p (m t b) -> p t m b", t=PACK, b=2)
+        )
 
         z = {t: sb.tile([P, S], F32, name=f"z{t}", align_bytes=64, tag=f"z{t}") for t in ORDER[:3]}
 
@@ -109,18 +129,21 @@ def tile_picked_modtrue_silu_po_kernel(
                 out=acc[:], lhsT=w1c[e][:, cols].bitcast(FP8X4), lhsT_scale=w1s[e][:, cols],
                 rhs=xwg[:, tok].bitcast(FP8X4), rhs_scale=xsp[:, tok], start=True, stop=True,
             )
-            nc.scalar.copy(z[t][:, tok], acc[:])
+            if (t, tok.start) == (first, 2 * CH):
+                nc.vector.tensor_copy(z[t][:, tok], acc[:])
+            else:
+                nc.scalar.copy(z[t][:, tok], acc[:])
 
         zq = [sb.tile([P, 2 * CH, PACK], BF16, name=f"zq{h}", align_bytes=64) for h in range(2)]
         act = {}
 
         def gather(t):
-            if t == ORDER[0]:
+            if t == first:
                 g = reuse.tile([P, V], F32, name=f"g{t}", align_bytes=64, offset=4 * T)
             else:
                 g = sb.tile([P, V], F32, name=f"g{t}", align_bytes=64)
             nc.vector.tensor_copy(g[:], z[t][:].indirect(take_t[:]))
-            a = sb.tile([P, V], F32, name=f"a{t}", align_bytes=64, tag=f"z{ORDER[0]}" if t == ORDER[-1] else f"a{t}")
+            a = sb.tile([P, V], F32, name=f"a{t}", align_bytes=64, tag=f"z{first}" if t == last else f"a{t}")
             nc.scalar.activation(a[:], g[:], SILU)
             act[t] = a
 
@@ -131,15 +154,15 @@ def tile_picked_modtrue_silu_po_kernel(
             for h in range(2):
                 nc.scalar.copy(zq[h][:, :, t], z[t][:, 2 * CH * h : 2 * CH * (h + 1)])
 
-        first, second, third, last = ORDER
+        layer1(first, slice(0, 2 * CH), 0)
+        layer1(first, slice(2 * CH, 3 * CH), 1)
+        layer1(first, slice(3 * CH, S), 2)
         for h in range(2):
-            tok = slice(h * S // 2, (h + 1) * S // 2)
-            layer1(first, tok, 2 * h)
-            layer1(second, tok, 2 * h + 1)
-        layer1(third, slice(0, S), 4)
+            layer1(second, slice(h * S // 2, (h + 1) * S // 2), 3 + h)
+        layer1(third, slice(0, S), 5)
         gather(first)
         z[last] = reuse.tile([P, S], F32, name="z_last", align_bytes=64, offset=4 * T)
-        layer1(last, slice(0, S), 5)
+        layer1(last, slice(0, S), 6)
         gather(second)
         gather(third)
         scatter(first)
@@ -165,24 +188,27 @@ def tile_picked_modtrue_silu_po_kernel(
         osc = sb.tile([P, S], U8, name="osc", align_bytes=64)
         out_rows = out_0.rearrange("(p t) j -> p t j", t=PACK)
         o32 = [sb.tile([P, PACK, hi - lo], F32, name=f"o32_{lo}", align_bytes=64) for lo, hi in SPANS]
-        nbank = 0
-        for c, (lo, hi) in enumerate(SPANS):
-            per = 2 * CH // (hi - lo)
-            for t0 in range(0, PACK, per):
-                bank = ps.tile([P, per, hi - lo], F32, name=f"o_acc{nbank}", tag=f"bank{nbank}")
-                nbank += 1
-                for i in range(per):
-                    t = t0 + i
-                    nc.tensor.matmul_mx(
-                        out=bank[:, i, :], lhsT=w2wd[:, 2 * P * t : 2 * P * (t + 1)].bitcast(FP4X4),
-                        lhsT_scale=w2sp[:, P * t : P * (t + 1)],
-                        rhs=zc[c][:].bitcast(FP8X4), rhs_scale=zs[c][:], start=True, stop=True,
-                    )
-                nc.scalar.copy(o32[c][:, t0 : t0 + per, :], bank[:])
-                done = t0 + per
-                group = PACK if c == 1 else 2
-                if done % group == 0:
-                    nc.sync.dma_start(out_rows[:, done - group : done, lo:hi], o32[c][:, done - group : done, :])
+        oq = [sb.tile([P, CH * PACK], BF16, name=f"oq{k}", align_bytes=64) for k in range(NCH)]
+        banks = []
+
+        def product(c, planes, part=None):
+            lo, hi = SPANS[c]
+            cols = slice(0, hi - lo) if part is None else slice(part * CH, (part + 1) * CH)
+            width = cols.stop - cols.start
+            nb = len(banks)
+            bank = ps.tile([P, len(planes), width], F32, name=f"o_acc{nb}", tag=f"bank{nb % 8}")
+            banks.append(bank)
+            for i, t in enumerate(planes):
+                nc.tensor.matmul_mx(
+                    out=bank[:, i, :], lhsT=w2wd[:, 2 * P * t : 2 * P * (t + 1)].bitcast(FP4X4),
+                    lhsT_scale=w2sp[:, P * t : P * (t + 1)],
+                    rhs=zc[c][:, cols].bitcast(FP8X4), rhs_scale=zs[c][:, cols], start=True, stop=True,
+                )
+            nc.scalar.copy(o32[c][:, planes[0] : planes[-1] + 1, cols], bank[:])
+
+        def store(c, t0, t1):
+            lo, hi = SPANS[c]
+            nc.sync.dma_start(out_rows[:, t0:t1, lo:hi], o32[c][:, t0:t1, :])
 
         def regroup(dst, c, part, ts):
             nc.vector.tensor_copy(
@@ -197,16 +223,31 @@ def tile_picked_modtrue_silu_po_kernel(
         def store_words(cols):
             nc.sync.dma_start(out_1[0, :, cols, :].rearrange("p c r -> p (c r)").bitcast(I32), ow[:, cols].bitcast(I32))
 
-        oq = [sb.tile([P, CH * PACK], BF16, name=f"oq{k}", align_bytes=64) for k in range(NCH)]
+        product(0, (0,))
+        store(0, 0, 1)
+        product(0, (1,))
+        product(0, (2, 3))
+        store(0, 1, 4)
+        product(1, (0, 1))
+        store(1, 0, 2)
+        product(1, (2, 3))
+        store(1, 2, 4)
+        product(2, (0,))
+        product(2, (1,))
+        store(2, 0, 2)
+        product(2, (2, 3), 0)
+        product(2, (2,), 1)
+        product(2, (3,), 1)
+        store(2, 2, 4)
         for c in range(2):
             regroup(oq[c], c, 0, slice(0, PACK))
             quantise_out(c)
         store_words(slice(0, 2 * CH))
-        for ts in (slice(0, 2), slice(2, PACK)):
-            for part in range(2):
-                regroup(oq[2 + part], 2, part, ts)
-        for part in range(2):
-            quantise_out(2 + part)
+        regroup(oq[3], 2, 1, slice(0, 2))
+        regroup(oq[2], 2, 0, slice(0, PACK))
+        quantise_out(2)
+        regroup(oq[3], 2, 1, slice(2, PACK))
+        quantise_out(3)
         store_words(slice(2 * CH, S))
         for q in range(QUADS):
             eng = nc.sync if q % 2 else nc.scalar

@@ -24,7 +24,7 @@ CH = 128
 NCH = S // CH
 SPANS = ((0, CH), (CH, 2 * CH), (2 * CH, S))
 ORDER = (2, 0, 1, 3)
-X_HEAD = T // 4
+X_HEAD = 3 * T // 8
 
 
 def tile_picked_modtrue_silu_po_kernel(
@@ -61,8 +61,8 @@ def tile_picked_modtrue_silu_po_kernel(
         nc.sync.dma_start(xw[:, :X_HEAD].bitcast(I32), x_rows[:, :X_HEAD])
         nc.sync.dma_start(offs_t[:], offs)
         nc.sync.dma_start(xs[0:P:8, :].bitcast(I32), x_scales[0].bitcast(I32))
-        nc.sync.dma_start(w2s[0:P:8, :].bitcast(I32), w2_scales[0].bitcast(I32))
         nc.sync.dma_start(xw[:, X_HEAD:].bitcast(I32), x_rows[:, X_HEAD:])
+        nc.sync.dma_start(w2s[0:P:8, :].bitcast(I32), w2_scales[0].bitcast(I32))
         nc.sync.dma_start(w1raw[0][:], w1_rows[:, 0:2, :])
         for j in range(2):
             nc.sync.dma_start(w1raw[1][:, j, :], w1_rows[:, 2 + j, :])
@@ -77,14 +77,20 @@ def tile_picked_modtrue_silu_po_kernel(
         nc.sync.dma_start(w2w[:].bitcast(I32), w2_words[0].bitcast(I32))
         nc.sync.dma_start(gate[:], wt.rearrange("(p j) v -> p j v", j=PACK)[:, 0, :])
 
+        xwg = sb.tile([P, S], U32, name="xwg", align_bytes=64)
+        nc.vector.tensor_copy(xwg[:], xw[:].indirect(offs_t[:]))
+
         w2sd = sb.tile([P, N], U8, name="w2sd", align_bytes=64)
         nc.vector.tensor_copy(w2sd[:].rearrange("p (t m) -> p t m", t=PACK), w2s[:].rearrange("p (m t) -> p t m", t=PACK))
         for q in range(QUADS):
             nc.sync.dma_start(w2sp[32 * q : 32 * q + 4, :].bitcast(I32), w2sd[32 * q : 32 * q + 32 : 8, :].bitcast(I32))
 
-        xwg = sb.tile([P, S], U32, name="xwg", align_bytes=64)
-        nc.vector.tensor_copy(xwg[:], xw[:].indirect(offs_t[:]))
-
+        for bank in (6, 7):
+            idle = ps.tile([P, S], F32, name=f"warm{bank}", tag=f"bank{bank}")
+            nc.tensor.matmul_mx(
+                out=idle[:], lhsT=xwg[:, :P].bitcast(FP8X4), lhsT_scale=xsg[:, :P],
+                rhs=xwg[:].bitcast(FP8X4), rhs_scale=xsg[:], start=True, stop=True,
+            )
         w1c = [sb.tile([P, 2 * P], U32, name=f"w1c{e}", align_bytes=64) for e in range(2)]
         w1s = [sb.tile([P, 2 * P], U8, name=f"w1s{e}", align_bytes=64) for e in range(2)]
         w1g = [reuse.tile([P, 2 * P * PACK], BF16, name="w1g0", align_bytes=64, offset=0),

@@ -22,7 +22,6 @@ PACK = 4
 QUADS = 4
 CH = 128
 NCH = S // CH
-SPANS = ((0, CH), (CH, 2 * CH), (2 * CH, S))
 ORDER = (2, 0, 1, 3)
 X_HEAD = 3 * T // 8
 
@@ -122,7 +121,7 @@ def tile_picked_modtrue_silu_po_kernel(
 
         w2wd = reuse.tile([P, 2 * N], U8, name="w2wd", align_bytes=64, offset=0)
         nc.vector.tensor_copy(
-            w2wd[:].rearrange("p (t m b) -> p t m b", t=PACK, b=2), w2w[:].rearrange("p (m t b) -> p t m b", t=PACK, b=2)
+            w2wd[:].bitcast(U16).rearrange("p (t m) -> p t m", t=PACK), w2w[:].bitcast(U16).rearrange("p (m t) -> p t m", t=PACK)
         )
 
         z = {t: sb.tile([P, S], F32, name=f"z{t}", align_bytes=64, tag=f"z{t}") for t in ORDER[:3]}
@@ -180,81 +179,87 @@ def tile_picked_modtrue_silu_po_kernel(
         weave(third)
         scatter(last)
 
-        zc = [sb.tile([P, hi - lo], U32, name=f"zc{lo}", align_bytes=64) for lo, hi in SPANS]
-        zs = [sb.tile([P, hi - lo], U8, name=f"zs{lo}", align_bytes=64) for lo, hi in SPANS]
+        half = 2 * CH
+        zc = [sb.tile([P, half], U32, name=f"zc{h}", align_bytes=64) for h in range(2)]
+        zs = [sb.tile([P, half], U8, name=f"zs{h}", align_bytes=64) for h in range(2)]
+
+        def weave_last(eng, c):
+            h, part = divmod(c, 2)
+            eng(zq[h][:, part * CH : (part + 1) * CH, last], z[last][:, c * CH : (c + 1) * CH])
+
+        weave_last(nc.vector.tensor_copy, 0)
+        weave_last(nc.vector.tensor_copy, 1)
+        weave_last(nc.scalar.copy, 3)
         for c in range(2):
-            nc.vector.tensor_copy(zq[0][:, c * CH : (c + 1) * CH, last], z[last][:, c * CH : (c + 1) * CH])
-        nc.scalar.copy(zq[1][:, :, last], z[last][:, 2 * CH : S])
-        for c in range(2):
-            src = zq[0][:, c * CH : (c + 1) * CH, :]
-            nc.vector.quantize_mx(out=zc[c][:].bitcast(FP8X4), scales=zs[c][:], in_=src.rearrange("p n j -> p (n j)"))
-        nc.vector.quantize_mx(out=zc[2][:].bitcast(FP8X4), scales=zs[2][:], in_=zq[1][:].rearrange("p n j -> p (n j)"))
+            cols = slice(c * CH, (c + 1) * CH)
+            nc.vector.quantize_mx(
+                out=zc[0][:, cols].bitcast(FP8X4), scales=zs[0][:, cols], in_=zq[0][:, cols, :].rearrange("p n j -> p (n j)")
+            )
+        weave_last(nc.vector.tensor_copy, 2)
+        nc.vector.quantize_mx(out=zc[1][:].bitcast(FP8X4), scales=zs[1][:], in_=zq[1][:].rearrange("p n j -> p (n j)"))
 
         ow = sb.tile([P, S], U32, name="ow", align_bytes=64)
         osc = sb.tile([P, S], U8, name="osc", align_bytes=64)
         out_rows = out_0.rearrange("(p t) j -> p t j", t=PACK)
-        o32 = [sb.tile([P, PACK, hi - lo], F32, name=f"o32_{lo}", align_bytes=64) for lo, hi in SPANS]
-        oq = [sb.tile([P, CH * PACK], BF16, name=f"oq{k}", align_bytes=64) for k in range(NCH)]
+        o32 = sb.tile([P, PACK, S], F32, name="o32", align_bytes=64)
+        oq01 = sb.tile([P, 2, CH * PACK], BF16, name="oq01", align_bytes=64)
+        oq = [oq01[:, 0, :], oq01[:, 1, :]] + [sb.tile([P, CH * PACK], BF16, name=f"oq{k}", align_bytes=64)[:] for k in (2, 3)]
         banks = []
 
-        def product(c, planes, part=None):
-            lo, hi = SPANS[c]
-            cols = slice(0, hi - lo) if part is None else slice(part * CH, (part + 1) * CH)
-            width = cols.stop - cols.start
+        def product(planes, lo, hi):
+            h = lo // half
+            cols = slice(lo - h * half, hi - h * half)
             nb = len(banks)
-            bank = ps.tile([P, len(planes), width], F32, name=f"o_acc{nb}", tag=f"bank{nb % 8}")
+            bank = ps.tile([P, len(planes), hi - lo], F32, name=f"o_acc{nb}", tag=f"bank{nb % 8}")
             banks.append(bank)
             for i, t in enumerate(planes):
                 nc.tensor.matmul_mx(
                     out=bank[:, i, :], lhsT=w2wd[:, 2 * P * t : 2 * P * (t + 1)].bitcast(FP4X4),
                     lhsT_scale=w2sp[:, P * t : P * (t + 1)],
-                    rhs=zc[c][:, cols].bitcast(FP8X4), rhs_scale=zs[c][:, cols], start=True, stop=True,
+                    rhs=zc[h][:, cols].bitcast(FP8X4), rhs_scale=zs[h][:, cols], start=True, stop=True,
                 )
-            nc.scalar.copy(o32[c][:, planes[0] : planes[-1] + 1, cols], bank[:])
+            nc.scalar.copy(o32[:, planes[0] : planes[-1] + 1, lo:hi], bank[:])
 
-        def store(c, t0, t1):
-            lo, hi = SPANS[c]
-            nc.sync.dma_start(out_rows[:, t0:t1, lo:hi], o32[c][:, t0:t1, :])
+        def store(t0, t1, lo, hi):
+            nc.sync.dma_start(out_rows[:, t0:t1, lo:hi], o32[:, t0:t1, lo:hi])
 
-        def regroup(dst, c, part, ts):
+        def regroup(c, ts):
             nc.vector.tensor_copy(
-                dst[:].rearrange("p (n i t) -> p n t i", i=4, t=PACK)[:, :, ts],
-                o32[c][:, ts, part * CH : (part + 1) * CH].rearrange("p t (n i) -> p n t i", i=4),
+                oq[c].rearrange("p (n i t) -> p n t i", i=4, t=PACK)[:, :, ts],
+                o32[:, ts, c * CH : (c + 1) * CH].rearrange("p t (n i) -> p n t i", i=4),
             )
 
         def quantise_out(k):
             cols = slice(k * CH, (k + 1) * CH)
-            nc.vector.quantize_mx(out=ow[:, cols].bitcast(FP8X4), scales=osc[:, cols], in_=oq[k][:])
+            nc.vector.quantize_mx(out=ow[:, cols].bitcast(FP8X4), scales=osc[:, cols], in_=oq[k])
 
         def store_words(cols):
             nc.sync.dma_start(out_1[0, :, cols, :].rearrange("p c r -> p (c r)").bitcast(I32), ow[:, cols].bitcast(I32))
 
-        product(0, (0,))
-        store(0, 0, 1)
-        product(0, (1,))
-        product(0, (2, 3))
-        store(0, 1, 4)
-        product(1, (0, 1))
-        store(1, 0, 2)
-        product(1, (2, 3))
-        store(1, 2, 4)
-        product(2, (0,))
-        product(2, (1,))
-        store(2, 0, 2)
-        product(2, (2, 3), 0)
-        product(2, (2,), 1)
-        product(2, (3,), 1)
-        store(2, 2, 4)
-        for c in range(2):
-            regroup(oq[c], c, 0, slice(0, PACK))
-            quantise_out(c)
-        store_words(slice(0, 2 * CH))
-        regroup(oq[3], 2, 1, slice(0, 2))
-        regroup(oq[2], 2, 0, slice(0, PACK))
+        product((0,), 0, CH)
+        store(0, 1, 0, CH)
+        for t in (1, 2, 3):
+            product((t,), 0, half)
+            store(t, t + 1, 0, half)
+        product((0,), CH, half)
+        regroup(0, slice(0, PACK))
+        regroup(1, slice(0, PACK))
+        nc.vector.quantize_mx(out=ow[:, :half].bitcast(FP8X4), scales=osc[:, :half], in_=oq01[:].rearrange("p c n -> p (c n)"))
+        product((0,), half, S)
+        store(0, 1, CH, S)
+        product((1,), half, S)
+        store(1, 2, half, S)
+        store_words(slice(0, half))
+        product((2, 3), half, 3 * CH)
+        regroup(3, slice(0, 2))
+        regroup(2, slice(0, PACK))
+        product((2,), 3 * CH, S)
+        product((3,), 3 * CH, S)
+        store(2, 4, half, S)
         quantise_out(2)
-        regroup(oq[3], 2, 1, slice(2, PACK))
+        regroup(3, slice(2, PACK))
         quantise_out(3)
-        store_words(slice(2 * CH, S))
+        store_words(slice(half, S))
         for q in range(QUADS):
             eng = nc.sync if q % 2 else nc.scalar
             eng.dma_start(out_2[0, 4 * q : 4 * q + 4, :].bitcast(I32), osc[32 * q : 32 * q + 4, :].bitcast(I32))

@@ -159,15 +159,15 @@ def tile_picked_modtrue_silu_po_kernel(
             for h in range(2):
                 nc.scalar.copy(zq[h][:, :, t], z[t][:, 2 * CH * h : 2 * CH * (h + 1)])
 
-        layer1(first, slice(0, 2 * CH), 0)
-        layer1(first, slice(2 * CH, 3 * CH), 1)
-        layer1(first, slice(3 * CH, S), 2)
-        for h in range(2):
-            layer1(second, slice(h * S // 2, (h + 1) * S // 2), 3 + h)
-        layer1(third, slice(0, S), 5)
+        for c in range(NCH):
+            layer1(first, slice(c * CH, (c + 1) * CH), c)
+        for i, t in enumerate((second, third)):
+            for h in range(2):
+                layer1(t, slice(h * S // 2, (h + 1) * S // 2), NCH + 2 * i + h)
         gather(first)
         z[last] = reuse.tile([P, S], F32, name="z_last", align_bytes=64, offset=4 * T)
-        layer1(last, slice(0, S), 6)
+        for h in range(2):
+            layer1(last, slice(h * S // 2, (h + 1) * S // 2), h)
         gather(second)
         gather(third)
         scatter(first)

@@ -202,8 +202,7 @@ def tile_picked_modtrue_silu_po_kernel(
         osc = sb.tile([P, S], U8, name="osc", align_bytes=64)
         out_rows = out_0.rearrange("(p t) j -> p t j", t=PACK)
         o32 = sb.tile([P, PACK, S], F32, name="o32", align_bytes=64)
-        oq01 = sb.tile([P, 2, CH * PACK], BF16, name="oq01", align_bytes=64)
-        oq = [oq01[:, 0, :], oq01[:, 1, :]] + [sb.tile([P, CH * PACK], BF16, name=f"oq{k}", align_bytes=64)[:] for k in (2, 3)]
+        oq = [sb.tile([P, CH * PACK], BF16, name=f"oq{k}", align_bytes=64) for k in range(NCH)]
         banks = []
 
         def product(planes, lo, hi):
@@ -223,15 +222,15 @@ def tile_picked_modtrue_silu_po_kernel(
         def store(t0, t1, lo, hi):
             nc.sync.dma_start(out_rows[:, t0:t1, lo:hi], o32[:, t0:t1, lo:hi])
 
-        def regroup(c, ts):
+        def regroup(c):
             nc.vector.tensor_copy(
-                oq[c].rearrange("p (n i t) -> p n t i", i=4, t=PACK)[:, :, ts],
-                o32[:, ts, c * CH : (c + 1) * CH].rearrange("p t (n i) -> p n t i", i=4),
+                oq[c][:].rearrange("p (n i t) -> p n t i", i=4, t=PACK),
+                o32[:, :, c * CH : (c + 1) * CH].rearrange("p t (n i) -> p n t i", i=4),
             )
 
         def quantise_out(k):
             cols = slice(k * CH, (k + 1) * CH)
-            nc.vector.quantize_mx(out=ow[:, cols].bitcast(FP8X4), scales=osc[:, cols], in_=oq[k])
+            nc.vector.quantize_mx(out=ow[:, cols].bitcast(FP8X4), scales=osc[:, cols], in_=oq[k][:])
 
         def store_words(cols):
             nc.sync.dma_start(out_1[0, :, cols, :].rearrange("p c r -> p (c r)").bitcast(I32), ow[:, cols].bitcast(I32))
@@ -242,23 +241,23 @@ def tile_picked_modtrue_silu_po_kernel(
             product((t,), 0, half)
             store(t, t + 1, 0, half)
         product((0,), CH, half)
-        regroup(0, slice(0, PACK))
-        regroup(1, slice(0, PACK))
-        nc.vector.quantize_mx(out=ow[:, :half].bitcast(FP8X4), scales=osc[:, :half], in_=oq01[:].rearrange("p c n -> p (c n)"))
+        for c in (0, 1):
+            regroup(c)
+        for c in (0, 1):
+            quantise_out(c)
         product((0,), half, S)
         store(0, 1, CH, S)
         product((1,), half, S)
         store(1, 2, half, S)
         store_words(slice(0, half))
-        product((2, 3), half, 3 * CH)
-        regroup(3, slice(0, 2))
-        regroup(2, slice(0, PACK))
-        product((2,), 3 * CH, S)
+        product((2,), half, S)
+        product((3,), half, 3 * CH)
         product((3,), 3 * CH, S)
         store(2, 4, half, S)
-        quantise_out(2)
-        regroup(3, slice(2, PACK))
-        quantise_out(3)
+        for c in (2, 3):
+            regroup(c)
+        for c in (2, 3):
+            quantise_out(c)
         store_words(slice(half, S))
         for q in range(QUADS):
             eng = nc.sync if q % 2 else nc.scalar

@@ -126,14 +126,17 @@ def tile_picked_modtrue_silu_po_kernel(
 
         z = {t: sb.tile([P, S], F32, name=f"z{t}", align_bytes=64, tag=f"z{t}") for t in ORDER[:3]}
 
-        def layer1(t, tok, bank):
+        def layer1(t, tok, bank, passes=1):
             u, e = divmod(t, 2)
             cols = slice(P * u, P * (u + 1))
-            acc = ps.tile([P, tok.stop - tok.start], F32, name=f"y_acc{bank}", tag=f"bank{bank}")
-            nc.tensor.matmul_mx(
-                out=acc[:], lhsT=w1c[e][:, cols].bitcast(FP8X4), lhsT_scale=w1s[e][:, cols],
-                rhs=xwg[:, tok].bitcast(FP8X4), rhs_scale=xsp[:, tok], start=True, stop=True,
-            )
+            width = tok.stop - tok.start
+            acc = ps.tile([P, width], F32, name=f"y_acc{bank}", tag=f"bank{bank}")
+            for lo in range(0, width, width // passes):
+                part = slice(tok.start + lo, tok.start + lo + width // passes)
+                nc.tensor.matmul_mx(
+                    out=acc[:, lo : lo + width // passes], lhsT=w1c[e][:, cols].bitcast(FP8X4), lhsT_scale=w1s[e][:, cols],
+                    rhs=xwg[:, part].bitcast(FP8X4), rhs_scale=xsp[:, part], start=True, stop=True,
+                )
             if (t, tok.start) == (first, 2 * CH):
                 nc.vector.tensor_copy(z[t][:, tok], acc[:])
             else:
@@ -159,15 +162,15 @@ def tile_picked_modtrue_silu_po_kernel(
             for h in range(2):
                 nc.scalar.copy(zq[h][:, :, t], z[t][:, 2 * CH * h : 2 * CH * (h + 1)])
 
-        for c in range(NCH):
-            layer1(first, slice(c * CH, (c + 1) * CH), c)
-        for i, t in enumerate((second, third)):
-            for h in range(2):
-                layer1(t, slice(h * S // 2, (h + 1) * S // 2), NCH + 2 * i + h)
+        layer1(first, slice(0, 2 * CH), 0)
+        layer1(first, slice(2 * CH, 3 * CH), 1)
+        layer1(first, slice(3 * CH, S), 2)
+        for h in range(2):
+            layer1(second, slice(h * S // 2, (h + 1) * S // 2), 3 + h)
+        layer1(third, slice(0, S), 5)
         gather(first)
         z[last] = reuse.tile([P, S], F32, name="z_last", align_bytes=64, offset=4 * T)
-        for h in range(2):
-            layer1(last, slice(h * S // 2, (h + 1) * S // 2), h)
+        layer1(last, slice(0, S), 6, passes=NCH)
         gather(second)
         gather(third)
         scatter(first)

@@ -15,6 +15,7 @@ U8 = mybir.dt.uint8
 FP8X4 = mybir.dt.float8_e4m3fn_x4
 FP4X4 = mybir.dt.float4_e2m1fn_x4
 SILU = mybir.ActivationFunctionType.Silu
+COPY = mybir.ActivationFunctionType.Copy
 MULT = mybir.AluOpType.mult
 
 P = 128
@@ -124,7 +125,7 @@ def tile_picked_modtrue_silu_po_kernel(
             w2wd[:].bitcast(U16).rearrange("p (t m) -> p t m", t=PACK), w2w[:].bitcast(U16).rearrange("p (m t) -> p t m", t=PACK)
         )
 
-        z = {t: sb.tile([P, S], F32, name=f"z{t}", align_bytes=64, tag=f"z{t}") for t in ORDER[:3]}
+        z = {t: sb.tile([P, S], F32, name=f"z{t}", align_bytes=64, tag=f"z{t}") for t in (first, second)}
 
         def layer1(t, tok, bank, passes=1):
             u, e = divmod(t, 2)
@@ -142,63 +143,80 @@ def tile_picked_modtrue_silu_po_kernel(
             else:
                 nc.scalar.copy(z[t][:, tok], acc[:])
 
-        zq = [sb.tile([P, 2 * CH, PACK], BF16, name=f"zq{h}", align_bytes=64) for h in range(2)]
-        act = {}
+        half = 2 * CH
+        zq = [sb.tile([P, half, PACK], BF16, name=f"zq{h}", align_bytes=64) for h in range(2)]
+        zp = sb.tile([P, 2, half, 2], BF16, name="zp", align_bytes=64)
+        picked, act = {}, {}
+        held = {first: 4 * T, second: 5 * T}
 
         def gather(t):
-            if t == first:
-                g = reuse.tile([P, V], F32, name=f"g{t}", align_bytes=64, offset=4 * T)
+            if t in held:
+                g = reuse.tile([P, V], F32, name=f"g{t}", align_bytes=64, offset=held[t])
+                nc.vector.tensor_copy(g[:], z[t][:].indirect(take_t[:]))
             else:
                 g = sb.tile([P, V], F32, name=f"g{t}", align_bytes=64)
-            nc.vector.tensor_copy(g[:], z[t][:].indirect(take_t[:]))
-            a = sb.tile([P, V], F32, name=f"a{t}", align_bytes=64, tag=f"z{first}" if t == last else f"a{t}")
-            nc.scalar.activation(a[:], g[:], SILU)
-            act[t] = a
+                nc.scalar.activation(g[:], z[t][:].indirect(take_t[:]), COPY)
+            picked[t] = g
 
-        def scatter(t):
-            nc.vector.tensor_tensor(z[t][:].indirect(take_t[:]), act[t][:], gate[:], MULT)
+        def silu(t, lo=0, hi=V, tag=None):
+            a = sb.tile([P, hi - lo], F32, name=f"a{t}_{lo}", align_bytes=64, tag=tag or f"a{t}_{lo}")
+            nc.scalar.activation(a[:], picked[t][:, lo:hi], SILU)
+            act[t, lo] = a
 
-        def weave(t):
-            for h in range(2):
-                nc.scalar.copy(zq[h][:, :, t], z[t][:, 2 * CH * h : 2 * CH * (h + 1)])
+        def scatter(t, lo=0, hi=V):
+            nc.vector.tensor_tensor(z[t][:].indirect(take_t[:, lo // 16 : hi // 16]), act[t, lo][:], gate[:, lo:hi], MULT)
+
+        def weave_low(eng, t, lo, hi):
+            eng(zq[0][:, lo:hi, t], z[t][:, lo:hi])
+
+        def weave_high(eng, t):
+            eng(zp[:, t // 2, :, t % 2], z[t][:, half:])
 
         layer1(first, slice(0, 2 * CH), 0)
         layer1(first, slice(2 * CH, 3 * CH), 1)
         layer1(first, slice(3 * CH, S), 2)
         for h in range(2):
             layer1(second, slice(h * S // 2, (h + 1) * S // 2), 3 + h)
-        layer1(third, slice(0, S), 5)
         gather(first)
-        z[last] = reuse.tile([P, S], F32, name="z_last", align_bytes=64, offset=4 * T)
-        layer1(last, slice(0, S), 6, passes=NCH)
+        silu(first)
         gather(second)
-        gather(third)
+        z[third] = reuse.tile([P, S], F32, name="z_third", align_bytes=64, offset=held[first])
+        layer1(third, slice(0, S), 5)
+        silu(second)
         scatter(first)
-        weave(first)
-        gather(last)
+        gather(third)
+        silu(third)
+        z[last] = reuse.tile([P, S], F32, name="z_last", align_bytes=64, offset=held[second])
+        layer1(last, slice(0, S), 6, passes=NCH)
         scatter(second)
-        weave(second)
+        gather(last)
+        silu(last, 0, V // 2)
+        weave_low(nc.scalar.copy, first, 0, half)
+        weave_high(nc.scalar.copy, first)
+        silu(last, V // 2, V, tag=f"z{first}")
         scatter(third)
-        weave(third)
-        scatter(last)
+        weave_low(nc.scalar.copy, second, 0, half)
+        weave_low(nc.scalar.copy, third, 0, half)
+        weave_high(nc.scalar.copy, second)
+        weave_high(nc.scalar.copy, third)
+        scatter(last, 0, V // 2)
+        scatter(last, V // 2, V)
 
-        half = 2 * CH
         zc = [sb.tile([P, half], U32, name=f"zc{h}", align_bytes=64) for h in range(2)]
         zs = [sb.tile([P, half], U8, name=f"zs{h}", align_bytes=64) for h in range(2)]
 
-        def weave_last(eng, c):
-            h, part = divmod(c, 2)
-            eng(zq[h][:, part * CH : (part + 1) * CH, last], z[last][:, c * CH : (c + 1) * CH])
-
-        weave_last(nc.vector.tensor_copy, 0)
-        weave_last(nc.vector.tensor_copy, 1)
-        weave_last(nc.scalar.copy, 3)
+        for c in range(2):
+            weave_low(nc.vector.tensor_copy, last, c * CH, (c + 1) * CH)
         for c in range(2):
             cols = slice(c * CH, (c + 1) * CH)
             nc.vector.quantize_mx(
                 out=zc[0][:, cols].bitcast(FP8X4), scales=zs[0][:, cols], in_=zq[0][:, cols, :].rearrange("p n j -> p (n j)")
             )
-        weave_last(nc.vector.tensor_copy, 2)
+        weave_high(nc.vector.tensor_copy, last)
+        nc.vector.tensor_copy(
+            zq[1][:].rearrange("p n j -> p (n j)").bitcast(I32).rearrange("p (n u) -> p n u", u=2),
+            zp[:].rearrange("p u n e -> p (u n e)").bitcast(I32).rearrange("p (u n) -> p n u", u=2),
+        )
         nc.vector.quantize_mx(out=zc[1][:].bitcast(FP8X4), scales=zs[1][:], in_=zq[1][:].rearrange("p n j -> p (n j)"))
 
         ow = sb.tile([P, S], U32, name="ow", align_bytes=64)

@@ -85,12 +85,6 @@ def tile_picked_modtrue_silu_po_kernel(
         for q in range(QUADS):
             nc.sync.dma_start(w2sp[32 * q : 32 * q + 4, :].bitcast(I32), w2sd[32 * q : 32 * q + 32 : 8, :].bitcast(I32))
 
-        for bank in (6, 7):
-            idle = ps.tile([P, S], F32, name=f"warm{bank}", tag=f"bank{bank}")
-            nc.tensor.matmul_mx(
-                out=idle[:], lhsT=xwg[:, :P].bitcast(FP8X4), lhsT_scale=xsg[:, :P],
-                rhs=xwg[:].bitcast(FP8X4), rhs_scale=xsg[:], start=True, stop=True,
-            )
         w1c = [sb.tile([P, 2 * P], U32, name=f"w1c{e}", align_bytes=64) for e in range(2)]
         w1s = [sb.tile([P, 2 * P], U8, name=f"w1s{e}", align_bytes=64) for e in range(2)]
         w1g = [reuse.tile([P, 2 * P * PACK], BF16, name="w1g0", align_bytes=64, offset=0),
@@ -127,58 +121,59 @@ def tile_picked_modtrue_silu_po_kernel(
 
         z = {t: sb.tile([P, S], F32, name=f"z{t}", align_bytes=64, tag=f"z{t}") for t in (first, second)}
 
-        def layer1(t, tok, bank, passes=1):
+        def layer1(t, tok, bank):
             u, e = divmod(t, 2)
             cols = slice(P * u, P * (u + 1))
             width = tok.stop - tok.start
             acc = ps.tile([P, width], F32, name=f"y_acc{bank}", tag=f"bank{bank}")
-            for lo in range(0, width, width // passes):
-                part = slice(tok.start + lo, tok.start + lo + width // passes)
-                nc.tensor.matmul_mx(
-                    out=acc[:, lo : lo + width // passes], lhsT=w1c[e][:, cols].bitcast(FP8X4), lhsT_scale=w1s[e][:, cols],
-                    rhs=xwg[:, part].bitcast(FP8X4), rhs_scale=xsp[:, part], start=True, stop=True,
-                )
+            nc.tensor.matmul_mx(
+                out=acc[:], lhsT=w1c[e][:, cols].bitcast(FP8X4), lhsT_scale=w1s[e][:, cols],
+                rhs=xwg[:, tok].bitcast(FP8X4), rhs_scale=xsp[:, tok], start=True, stop=True,
+            )
             if (t, tok.start) == (first, 2 * CH):
                 nc.vector.tensor_copy(z[t][:, tok], acc[:])
             else:
                 nc.scalar.copy(z[t][:, tok], acc[:])
 
         half = 2 * CH
-        zq = [sb.tile([P, half, PACK], BF16, name=f"zq{h}", align_bytes=64) for h in range(2)]
-        zp = sb.tile([P, 2, half, 2], BF16, name="zp", align_bytes=64)
+        zq = [sb.tile([P, n, PACK], BF16, name=f"zq{h}", align_bytes=64) for h, n in enumerate((half, CH, CH))]
+        zp = sb.tile([P, PACK, half], BF16, name="zp", align_bytes=64)
         picked, act = {}, {}
         held = {first: 4 * T, second: 5 * T}
 
-        def gather(t):
+        def gather(t, parts=1):
             if t in held:
                 g = reuse.tile([P, V], F32, name=f"g{t}", align_bytes=64, offset=held[t])
-                nc.vector.tensor_copy(g[:], z[t][:].indirect(take_t[:]))
+                for lo in range(0, V, V // parts):
+                    hi = lo + V // parts
+                    nc.vector.tensor_copy(g[:, lo:hi], z[t][:].indirect(take_t[:, lo // 16 : hi // 16]))
             else:
                 g = sb.tile([P, V], F32, name=f"g{t}", align_bytes=64)
                 nc.scalar.activation(g[:], z[t][:].indirect(take_t[:]), COPY)
             picked[t] = g
 
-        def silu(t, lo=0, hi=V, tag=None):
-            a = sb.tile([P, hi - lo], F32, name=f"a{t}_{lo}", align_bytes=64, tag=tag or f"a{t}_{lo}")
-            nc.scalar.activation(a[:], picked[t][:, lo:hi], SILU)
-            act[t, lo] = a
+        def silu(t, parts=1):
+            a = sb.tile([P, V], F32, name=f"a{t}", align_bytes=64)
+            for lo in range(0, V, V // parts):
+                nc.scalar.activation(a[:, lo : lo + V // parts], picked[t][:, lo : lo + V // parts], SILU)
+            act[t] = a
 
-        def scatter(t, lo=0, hi=V):
-            nc.vector.tensor_tensor(z[t][:].indirect(take_t[:, lo // 16 : hi // 16]), act[t, lo][:], gate[:, lo:hi], MULT)
+        def scatter(t):
+            nc.vector.tensor_tensor(z[t][:].indirect(take_t[:]), act[t][:], gate[:], MULT)
 
         def weave_low(eng, t, lo, hi):
             eng(zq[0][:, lo:hi, t], z[t][:, lo:hi])
 
         def weave_high(eng, t):
-            eng(zp[:, t // 2, :, t % 2], z[t][:, half:])
+            eng(zp[:, t, :], z[t][:, half:])
 
         layer1(first, slice(0, 2 * CH), 0)
         layer1(first, slice(2 * CH, 3 * CH), 1)
         layer1(first, slice(3 * CH, S), 2)
         for h in range(2):
             layer1(second, slice(h * S // 2, (h + 1) * S // 2), 3 + h)
-        gather(first)
-        silu(first)
+        gather(first, parts=2)
+        silu(first, parts=2)
         gather(second)
         z[third] = reuse.tile([P, S], F32, name="z_third", align_bytes=64, offset=held[first])
         layer1(third, slice(0, S), 5)
@@ -187,20 +182,18 @@ def tile_picked_modtrue_silu_po_kernel(
         gather(third)
         silu(third)
         z[last] = reuse.tile([P, S], F32, name="z_last", align_bytes=64, offset=held[second])
-        layer1(last, slice(0, S), 6, passes=NCH)
+        layer1(last, slice(0, S), 6)
         scatter(second)
         gather(last)
-        silu(last, 0, V // 2)
         weave_low(nc.scalar.copy, first, 0, half)
-        weave_high(nc.scalar.copy, first)
-        silu(last, V // 2, V, tag=f"z{first}")
+        silu(last)
         scatter(third)
         weave_low(nc.scalar.copy, second, 0, half)
         weave_low(nc.scalar.copy, third, 0, half)
+        weave_high(nc.scalar.copy, first)
         weave_high(nc.scalar.copy, second)
         weave_high(nc.scalar.copy, third)
-        scatter(last, 0, V // 2)
-        scatter(last, V // 2, V)
+        scatter(last)
 
         zc = [sb.tile([P, half], U32, name=f"zc{h}", align_bytes=64) for h in range(2)]
         zs = [sb.tile([P, half], U8, name=f"zs{h}", align_bytes=64) for h in range(2)]
@@ -212,12 +205,17 @@ def tile_picked_modtrue_silu_po_kernel(
             nc.vector.quantize_mx(
                 out=zc[0][:, cols].bitcast(FP8X4), scales=zs[0][:, cols], in_=zq[0][:, cols, :].rearrange("p n j -> p (n j)")
             )
-        weave_high(nc.vector.tensor_copy, last)
-        nc.vector.tensor_copy(
-            zq[1][:].rearrange("p n j -> p (n j)").bitcast(I32).rearrange("p (n u) -> p n u", u=2),
-            zp[:].rearrange("p u n e -> p (u n e)").bitcast(I32).rearrange("p (u n) -> p n u", u=2),
-        )
-        nc.vector.quantize_mx(out=zc[1][:].bitcast(FP8X4), scales=zs[1][:], in_=zq[1][:].rearrange("p n j -> p (n j)"))
+        weave_high(nc.scalar.copy, last)
+        for c in range(2):
+            nc.vector.tensor_copy(
+                zq[1 + c][:].rearrange("p (n i) t -> p n t i", i=4),
+                zp[:, :, c * CH : (c + 1) * CH].rearrange("p t (n i) -> p n t i", i=4),
+            )
+        for c in range(2):
+            cols = slice(c * CH, (c + 1) * CH)
+            nc.vector.quantize_mx(
+                out=zc[1][:, cols].bitcast(FP8X4), scales=zs[1][:, cols], in_=zq[1 + c][:].rearrange("p n j -> p (n j)")
+            )
 
         ow = sb.tile([P, S], U32, name="ow", align_bytes=64)
         osc = sb.tile([P, S], U8, name="osc", align_bytes=64)

@@ -119,7 +119,7 @@ def tile_picked_modtrue_silu_po_kernel(
             w2wd[:].bitcast(U16).rearrange("p (t m) -> p t m", t=PACK), w2w[:].bitcast(U16).rearrange("p (m t) -> p t m", t=PACK)
         )
 
-        z = {t: sb.tile([P, S], F32, name=f"z{t}", align_bytes=64, tag=f"z{t}") for t in (first, second)}
+        z = {t: sb.tile([P, S], F32, name=f"z{t}", align_bytes=64) for t in ORDER}
 
         def layer1(t, tok, bank):
             u, e = divmod(t, 2)
@@ -130,33 +130,22 @@ def tile_picked_modtrue_silu_po_kernel(
                 out=acc[:], lhsT=w1c[e][:, cols].bitcast(FP8X4), lhsT_scale=w1s[e][:, cols],
                 rhs=xwg[:, tok].bitcast(FP8X4), rhs_scale=xsp[:, tok], start=True, stop=True,
             )
-            if (t, tok.start) == (first, 2 * CH):
-                nc.vector.tensor_copy(z[t][:, tok], acc[:])
-            else:
-                nc.scalar.copy(z[t][:, tok], acc[:])
+            return acc
 
         half = 2 * CH
         zq = [sb.tile([P, n, PACK], BF16, name=f"zq{h}", align_bytes=64) for h, n in enumerate((half, CH, CH))]
         zp = sb.tile([P, PACK, half], BF16, name="zp", align_bytes=64)
-        picked, act = {}, {}
-        held = {first: 4 * T, second: 5 * T}
+        act = {t: sb.tile([P, V], F32, name=f"a{t}", align_bytes=64) for t in ORDER}
+        picked = {t: sb.tile([P, V], F32, name=f"g{t}", align_bytes=64) for t in ORDER[1:]}
 
         def gather(t, parts=1):
-            if t in held:
-                g = reuse.tile([P, V], F32, name=f"g{t}", align_bytes=64, offset=held[t])
-                for lo in range(0, V, V // parts):
-                    hi = lo + V // parts
-                    nc.vector.tensor_copy(g[:, lo:hi], z[t][:].indirect(take_t[:, lo // 16 : hi // 16]))
-            else:
-                g = sb.tile([P, V], F32, name=f"g{t}", align_bytes=64)
-                nc.scalar.activation(g[:], z[t][:].indirect(take_t[:]), COPY)
-            picked[t] = g
+            for lo in range(0, V, V // parts):
+                hi = lo + V // parts
+                nc.scalar.activation(picked[t][:, lo:hi], z[t][:].indirect(take_t[:, lo // 16 : hi // 16]), COPY)
 
         def silu(t, parts=1):
-            a = sb.tile([P, V], F32, name=f"a{t}", align_bytes=64)
             for lo in range(0, V, V // parts):
-                nc.scalar.activation(a[:, lo : lo + V // parts], picked[t][:, lo : lo + V // parts], SILU)
-            act[t] = a
+                nc.scalar.activation(act[t][:, lo : lo + V // parts], picked[t][:, lo : lo + V // parts], SILU)
 
         def scatter(t):
             nc.vector.tensor_tensor(z[t][:].indirect(take_t[:]), act[t][:], gate[:], MULT)
@@ -167,32 +156,32 @@ def tile_picked_modtrue_silu_po_kernel(
         def weave_high(eng, t):
             eng(zp[:, t, :], z[t][:, half:])
 
-        layer1(first, slice(0, 2 * CH), 0)
-        layer1(first, slice(2 * CH, 3 * CH), 1)
-        layer1(first, slice(3 * CH, S), 2)
+        halves = [slice(0, half), slice(half, S)]
+        lead = [layer1(first, halves[h], h) for h in range(2)]
+        lead_act = sb.tile([P, S], F32, name="lead_act", align_bytes=64)
         for h in range(2):
-            layer1(second, slice(h * S // 2, (h + 1) * S // 2), 3 + h)
-        gather(first, parts=2)
-        silu(first, parts=2)
-        gather(second)
-        z[third] = reuse.tile([P, S], F32, name="z_third", align_bytes=64, offset=held[first])
-        layer1(third, slice(0, S), 5)
-        silu(second)
+            nc.scalar.activation(lead_act[:, halves[h]], lead[h][:], SILU)
+        nc.vector.tensor_copy(z[first][:, halves[0]], lead[0][:])
+        nc.vector.tensor_copy(act[first][:], lead_act[:].indirect(take_t[:]))
+        for h in range(2):
+            nc.scalar.copy(z[second][:, halves[h]], layer1(second, halves[h], 2 + h)[:])
+        nc.scalar.copy(z[first][:, halves[1]], lead[1][:])
+        nc.vector.tensor_copy(picked[second][:], z[second][:].indirect(take_t[:]))
         scatter(first)
-        gather(third)
-        silu(third)
-        z[last] = reuse.tile([P, S], F32, name="z_last", align_bytes=64, offset=held[second])
-        layer1(last, slice(0, S), 6)
+        nc.scalar.copy(z[third][:], layer1(third, slice(0, S), 4)[:])
+        silu(second)
         scatter(second)
+        gather(third)
+        nc.scalar.copy(z[last][:], layer1(last, slice(0, S), 5)[:])
+        silu(third)
+        scatter(third)
         gather(last)
         weave_low(nc.scalar.copy, first, 0, half)
         silu(last)
-        scatter(third)
         weave_low(nc.scalar.copy, second, 0, half)
         weave_low(nc.scalar.copy, third, 0, half)
-        weave_high(nc.scalar.copy, first)
-        weave_high(nc.scalar.copy, second)
-        weave_high(nc.scalar.copy, third)
+        for t in (first, second, third):
+            weave_high(nc.scalar.copy, t)
         scatter(last)
 
         zc = [sb.tile([P, half], U32, name=f"zc{h}", align_bytes=64) for h in range(2)]

@@ -166,7 +166,7 @@ def tile_picked_modtrue_silu_po_kernel(
         for h in range(2):
             nc.scalar.copy(z[second][:, halves[h]], layer1(second, halves[h], 2 + h)[:])
         nc.scalar.copy(z[first][:, halves[1]], lead[1][:])
-        nc.vector.tensor_copy(picked[second][:], z[second][:].indirect(take_t[:]))
+        gather(second)
         scatter(first)
         nc.scalar.copy(z[third][:], layer1(third, slice(0, S), 4)[:])
         silu(second)

@@ -24,7 +24,7 @@ QUADS = 4
 CH = 128
 NCH = S // CH
 ORDER = (2, 0, 1, 3)
-X_HEAD = 3 * T // 8
+W_HEAD = 3 * PACK * H // 8
 
 
 def tile_picked_modtrue_silu_po_kernel(
@@ -41,13 +41,13 @@ def tile_picked_modtrue_silu_po_kernel(
         offs_t = sb.tile([P, S // 16], U16, name="offs_t")
         take_t = sb.tile([P, V // 16], U16, name="take_t")
         xw = sb.tile([P, T], U32, name="xw", align_bytes=64)
-        xs = late.tile([P, T], U8, name="xs", align_bytes=64, offset=0)
+        xs = sb.tile([P, T], U8, name="xs", align_bytes=64)
         w2s = sb.tile([P, N], U8, name="w2s", align_bytes=64)
         xsp = sb.tile([P, S], U8, name="xsp", align_bytes=64)
         w2sp = sb.tile([P, N], U8, name="w2sp", align_bytes=64)
         warm_in = sb.tile([P, 8], F32, name="warm_in")
         warm_out = sb.tile([P, 8], F32, name="warm_out")
-        w1raw = [sb.tile([P, 2, H], F32, name=f"w1raw{a}", align_bytes=64) for a in range(2)]
+        w1raw = late.tile([P, PACK * H], F32, name="w1raw", align_bytes=64, offset=0)
 
         nc.vector.memset(xs[:].bitcast(I32), 0)
         nc.vector.memset(w2s[:].bitcast(I32), 0)
@@ -57,95 +57,69 @@ def tile_picked_modtrue_silu_po_kernel(
         nc.scalar.activation(warm_out[:], warm_in[:], SILU)
 
         x_rows = x_words[0].rearrange("p c r -> p (c r)").bitcast(I32)
-        w1_rows = w1.rearrange("(p j) c -> p j c", j=PACK)
-        nc.sync.dma_start(xw[:, :X_HEAD].bitcast(I32), x_rows[:, :X_HEAD])
+        w1_rows = w1.rearrange("(p j) c -> p (j c)", j=PACK)
+        nc.sync.dma_start(w1raw[:, :W_HEAD], w1_rows[:, :W_HEAD])
         nc.sync.dma_start(offs_t[:], offs)
         nc.sync.dma_start(xs[0:P:8, :].bitcast(I32), x_scales[0].bitcast(I32))
-        nc.sync.dma_start(xw[:, X_HEAD:].bitcast(I32), x_rows[:, X_HEAD:])
+        nc.sync.dma_start(w1raw[:, W_HEAD:], w1_rows[:, W_HEAD:])
+        nc.sync.dma_start(xw[:].bitcast(I32), x_rows)
         nc.sync.dma_start(w2s[0:P:8, :].bitcast(I32), w2_scales[0].bitcast(I32))
-        nc.sync.dma_start(w1raw[0][:], w1_rows[:, 0:2, :])
-        for j in range(2):
-            nc.sync.dma_start(w1raw[1][:, j, :], w1_rows[:, 2 + j, :])
+        w2w = sb.tile([P, 2 * N], U8, name="w2w", align_bytes=64)
+        nc.sync.dma_start(w2w[:].bitcast(I32), w2_words[0].bitcast(I32))
+        nc.sync.dma_start(take_t[:], take)
 
         xsg = sb.tile([P, S], U8, name="xsg", align_bytes=64)
         nc.vector.tensor_copy(xsg[:], xs[:].indirect(offs_t[:]))
         for q in range(QUADS):
             nc.scalar.dma_start(xsp[32 * q : 32 * q + 4, :].bitcast(I32), xsg[32 * q : 32 * q + 32 : 8, :].bitcast(I32))
-        nc.sync.dma_start(take_t[:], take)
-        w2w = late.tile([P, 2 * N], U8, name="w2w", align_bytes=64, offset=0)
-        gate = late.tile([P, V], F32, name="gate", align_bytes=64, offset=2 * N)
-        nc.sync.dma_start(w2w[:].bitcast(I32), w2_words[0].bitcast(I32))
+
+        w1c = sb.tile([P, H], U32, name="w1c", align_bytes=64)
+        w1s = sb.tile([P, H], U8, name="w1s", align_bytes=64)
+        w1g = sb.tile([P, H * PACK], BF16, name="w1g", align_bytes=64)
+        dealt = w1g[:].rearrange("p (t m j) -> p m j t", t=PACK, j=PACK)
+        plain = w1raw[:].rearrange("p (j m t) -> p m j t", j=PACK, t=PACK)
+        nc.vector.tensor_copy(dealt, plain)
+        gate = late.tile([P, V], F32, name="gate", align_bytes=64, offset=0)
         nc.sync.dma_start(gate[:], wt.rearrange("(p j) v -> p j v", j=PACK)[:, 0, :])
 
+        nc.vector.quantize_mx(out=w1c[:].bitcast(FP8X4), scales=w1s[:], in_=w1g[:])
+
+        half = 2 * CH
+        halves = [slice(0, half), slice(half, S)]
         xwg = sb.tile([P, S], U32, name="xwg", align_bytes=64)
-        nc.vector.tensor_copy(xwg[:], xw[:].indirect(offs_t[:]))
+        for h in range(2):
+            nc.vector.tensor_copy(xwg[:, halves[h]], xw[:].indirect(offs_t[:, h * half // 16 : (h + 1) * half // 16]))
 
         w2sd = sb.tile([P, N], U8, name="w2sd", align_bytes=64)
         nc.vector.tensor_copy(w2sd[:].rearrange("p (t m) -> p t m", t=PACK), w2s[:].rearrange("p (m t) -> p t m", t=PACK))
         for q in range(QUADS):
             nc.sync.dma_start(w2sp[32 * q : 32 * q + 4, :].bitcast(I32), w2sd[32 * q : 32 * q + 32 : 8, :].bitcast(I32))
-
-        w1c = [sb.tile([P, 2 * P], U32, name=f"w1c{e}", align_bytes=64) for e in range(2)]
-        w1s = [sb.tile([P, 2 * P], U8, name=f"w1s{e}", align_bytes=64) for e in range(2)]
-        w1g = [reuse.tile([P, 2 * P * PACK], BF16, name="w1g0", align_bytes=64, offset=0),
-               sb.tile([P, 2 * P * PACK], BF16, name="w1g1", align_bytes=64)]
-
-        def cast_views(a, e):
-            dst = w1g[e][:].rearrange("p (u m a j) -> p a u m j", u=2, a=2, j=2)[:, a]
-            src = w1raw[a][:].rearrange("p j (m u e) -> p e u m j", u=2, e=2)[:, e]
-            return dst, src
-
-        def cast_pair(eng, a, e):
-            dst, src = cast_views(a, e)
-            eng(dst.rearrange("p u m j -> p m u j"), src.rearrange("p u m j -> p m u j"))
-
-        cast_pair(nc.vector.tensor_copy, 0, 0)
-        cast_pair(nc.scalar.copy, 0, 1)
-        cast_pair(nc.scalar.copy, 1, 1)
-        dst, src = cast_views(1, 0)
-        nc.vector.tensor_copy(dst[:, :, :, 0].rearrange("p u m -> p m u"), src[:, :, :, 0].rearrange("p u m -> p m u"))
-        for t in (first, second):
-            nc.vector.tensor_copy(dst[:, t // 2, :, 1], src[:, t // 2, :, 1])
-        for t in (first, second):
-            u = t // 2
-            nc.vector.quantize_mx(
-                out=w1c[0][:, P * u : P * (u + 1)].bitcast(FP8X4), scales=w1s[0][:, P * u : P * (u + 1)],
-                in_=w1g[0][:, PACK * P * u : PACK * P * (u + 1)],
-            )
-        nc.vector.quantize_mx(out=w1c[1][:].bitcast(FP8X4), scales=w1s[1][:], in_=w1g[1][:])
-
-        w2wd = reuse.tile([P, 2 * N], U8, name="w2wd", align_bytes=64, offset=0)
-        nc.vector.tensor_copy(
+        w2wd = sb.tile([P, 2 * N], U8, name="w2wd", align_bytes=64)
+        nc.scalar.copy(
             w2wd[:].bitcast(U16).rearrange("p (t m) -> p t m", t=PACK), w2w[:].bitcast(U16).rearrange("p (m t) -> p t m", t=PACK)
         )
 
-        z = {t: sb.tile([P, S], F32, name=f"z{t}", align_bytes=64) for t in ORDER}
-
         def layer1(t, tok, bank):
-            u, e = divmod(t, 2)
-            cols = slice(P * u, P * (u + 1))
+            cols = slice(P * t, P * (t + 1))
             width = tok.stop - tok.start
             acc = ps.tile([P, width], F32, name=f"y_acc{bank}", tag=f"bank{bank}")
             nc.tensor.matmul_mx(
-                out=acc[:], lhsT=w1c[e][:, cols].bitcast(FP8X4), lhsT_scale=w1s[e][:, cols],
+                out=acc[:], lhsT=w1c[:, cols].bitcast(FP8X4), lhsT_scale=w1s[:, cols],
                 rhs=xwg[:, tok].bitcast(FP8X4), rhs_scale=xsp[:, tok], start=True, stop=True,
             )
             return acc
 
-        half = 2 * CH
+        z = {t: sb.tile([P, S], F32, name=f"z{t}", align_bytes=64) for t in (first, second, last)}
         zq = [sb.tile([P, n, PACK], BF16, name=f"zq{h}", align_bytes=64) for h, n in enumerate((half, CH, CH))]
         zp = sb.tile([P, PACK, half], BF16, name="zp", align_bytes=64)
         act = {t: sb.tile([P, V], F32, name=f"a{t}", align_bytes=64) for t in ORDER}
         picked = {t: sb.tile([P, V], F32, name=f"g{t}", align_bytes=64) for t in ORDER[1:]}
 
-        def gather(t, parts=1):
-            for lo in range(0, V, V // parts):
-                hi = lo + V // parts
-                nc.scalar.activation(picked[t][:, lo:hi], z[t][:].indirect(take_t[:, lo // 16 : hi // 16]), COPY)
+        def gather(t):
+            nc.scalar.activation(picked[t][:], z[t][:].indirect(take_t[:]), COPY)
 
-        def silu(t, parts=1):
-            for lo in range(0, V, V // parts):
-                nc.scalar.activation(act[t][:, lo : lo + V // parts], picked[t][:, lo : lo + V // parts], SILU)
+        def silu(t):
+            nc.scalar.activation(act[t][:], picked[t][:], SILU)
 
         def scatter(t):
             nc.vector.tensor_tensor(z[t][:].indirect(take_t[:]), act[t][:], gate[:], MULT)
@@ -156,18 +130,20 @@ def tile_picked_modtrue_silu_po_kernel(
         def weave_high(eng, t):
             eng(zp[:, t, :], z[t][:, half:])
 
-        halves = [slice(0, half), slice(half, S)]
-        lead = [layer1(first, halves[h], h) for h in range(2)]
-        lead_act = sb.tile([P, S], F32, name="lead_act", align_bytes=64)
+        lists = [slice(0, V // 32), slice(V // 32, V // 16)]
+        picks = [slice(0, V // 2), slice(V // 2, V)]
+        lead_act = reuse.tile([P, S], F32, name="lead_act", align_bytes=64, offset=0)
         for h in range(2):
-            nc.scalar.activation(lead_act[:, halves[h]], lead[h][:], SILU)
-        nc.vector.tensor_copy(z[first][:, halves[0]], lead[0][:])
-        nc.vector.tensor_copy(act[first][:], lead_act[:].indirect(take_t[:]))
-        for h in range(2):
-            nc.scalar.copy(z[second][:, halves[h]], layer1(second, halves[h], 2 + h)[:])
-        nc.scalar.copy(z[first][:, halves[1]], lead[1][:])
+            lead = layer1(first, halves[h], 2 * h)
+            follow = layer1(second, halves[h], 2 * h + 1)
+            nc.scalar.activation(lead_act[:, halves[h]], lead[:], SILU)
+            nc.scalar.copy(z[first][:, halves[h]], lead[:])
+            nc.vector.tensor_copy(z[second][:, halves[h]], follow[:])
+        nc.vector.tensor_copy(act[first][:, picks[0]], lead_act[:].indirect(take_t[:, lists[0]]))
+        nc.scalar.activation(act[first][:, picks[1]], lead_act[:].indirect(take_t[:, lists[1]]), COPY)
         gather(second)
         scatter(first)
+        z[third] = reuse.tile([P, S], F32, name="z_third", align_bytes=64, offset=0)
         nc.scalar.copy(z[third][:], layer1(third, slice(0, S), 4)[:])
         silu(second)
         scatter(second)

@@ -35,6 +35,7 @@ def tile_picked_modtrue_silu_po_kernel(
         sb = ctx.enter_context(tc.tile_pool(name="sb", bufs=1))
         reuse = ctx.enter_context(tc.tile_pool(name="reuse", bufs=1))
         late = ctx.enter_context(tc.tile_pool(name="late", bufs=1))
+        words = ctx.enter_context(tc.tile_pool(name="words", bufs=1))
         ps = ctx.enter_context(tc.psum_pool(name="ps", bufs=1))
         first, second, third, last = ORDER
 
@@ -64,8 +65,6 @@ def tile_picked_modtrue_silu_po_kernel(
         nc.sync.dma_start(w1raw[:, W_HEAD:], w1_rows[:, W_HEAD:])
         nc.sync.dma_start(xw[:].bitcast(I32), x_rows)
         nc.sync.dma_start(w2s[0:P:8, :].bitcast(I32), w2_scales[0].bitcast(I32))
-        w2w = sb.tile([P, 2 * N], U8, name="w2w", align_bytes=64)
-        nc.sync.dma_start(w2w[:].bitcast(I32), w2_words[0].bitcast(I32))
         nc.sync.dma_start(take_t[:], take)
 
         xsg = sb.tile([P, S], U8, name="xsg", align_bytes=64)
@@ -81,6 +80,8 @@ def tile_picked_modtrue_silu_po_kernel(
         nc.vector.tensor_copy(dealt, plain)
         gate = late.tile([P, V], F32, name="gate", align_bytes=64, offset=0)
         nc.sync.dma_start(gate[:], wt.rearrange("(p j) v -> p j v", j=PACK)[:, 0, :])
+        w2w = late.tile([P, 2 * N], U8, name="w2w", align_bytes=64, offset=4 * V)
+        nc.sync.dma_start(w2w[:].bitcast(I32), w2_words[0].bitcast(I32))
 
         nc.vector.quantize_mx(out=w1c[:].bitcast(FP8X4), scales=w1s[:], in_=w1g[:])
 
@@ -94,10 +95,6 @@ def tile_picked_modtrue_silu_po_kernel(
         nc.vector.tensor_copy(w2sd[:].rearrange("p (t m) -> p t m", t=PACK), w2s[:].rearrange("p (m t) -> p t m", t=PACK))
         for q in range(QUADS):
             nc.sync.dma_start(w2sp[32 * q : 32 * q + 4, :].bitcast(I32), w2sd[32 * q : 32 * q + 32 : 8, :].bitcast(I32))
-        w2wd = sb.tile([P, 2 * N], U8, name="w2wd", align_bytes=64)
-        nc.scalar.copy(
-            w2wd[:].bitcast(U16).rearrange("p (t m) -> p t m", t=PACK), w2w[:].bitcast(U16).rearrange("p (m t) -> p t m", t=PACK)
-        )
 
         def layer1(t, tok, bank):
             cols = slice(P * t, P * (t + 1))
@@ -111,9 +108,10 @@ def tile_picked_modtrue_silu_po_kernel(
 
         z = {t: sb.tile([P, S], F32, name=f"z{t}", align_bytes=64) for t in (first, second, last)}
         zq = [sb.tile([P, n, PACK], BF16, name=f"zq{h}", align_bytes=64) for h, n in enumerate((half, CH, CH))]
-        zp = sb.tile([P, PACK, half], BF16, name="zp", align_bytes=64)
+        zp = sb.tile([P, PACK, half], F32, name="zp", align_bytes=64)
         act = {t: sb.tile([P, V], F32, name=f"a{t}", align_bytes=64) for t in ORDER}
-        picked = {t: sb.tile([P, V], F32, name=f"g{t}", align_bytes=64) for t in ORDER[1:]}
+        picked = {t: sb.tile([P, V], F32, name=f"g{t}", align_bytes=64) for t in (second, third)}
+        picked[last] = words.tile([P, V], F32, name="g_last", align_bytes=64, offset=0)
 
         def gather(t):
             nc.scalar.activation(picked[t][:], z[t][:].indirect(take_t[:]), COPY)
@@ -155,9 +153,14 @@ def tile_picked_modtrue_silu_po_kernel(
         weave_low(nc.scalar.copy, first, 0, half)
         silu(last)
         weave_low(nc.scalar.copy, second, 0, half)
+        w2wd = words.tile([P, 2 * N], U8, name="w2wd", align_bytes=64, offset=0)
+        nc.scalar.copy(
+            w2wd[:].bitcast(U16).rearrange("p (t m) -> p t m", t=PACK), w2w[:].bitcast(U16).rearrange("p (m t) -> p t m", t=PACK)
+        )
         weave_low(nc.scalar.copy, third, 0, half)
-        for t in (first, second, third):
-            weave_high(nc.scalar.copy, t)
+        for t in (first, second):
+            weave_high(nc.sync.dma_start, t)
+        weave_high(nc.scalar.copy, third)
         scatter(last)
 
         zc = [sb.tile([P, half], U32, name=f"zc{h}", align_bytes=64) for h in range(2)]

@@ -36,12 +36,13 @@ def tile_picked_modtrue_silu_po_kernel(
         reuse = ctx.enter_context(tc.tile_pool(name="reuse", bufs=1))
         late = ctx.enter_context(tc.tile_pool(name="late", bufs=1))
         words = ctx.enter_context(tc.tile_pool(name="words", bufs=1))
+        rows = ctx.enter_context(tc.tile_pool(name="rows", bufs=1))
         ps = ctx.enter_context(tc.psum_pool(name="ps", bufs=1))
         first, second, third, last = ORDER
 
         offs_t = sb.tile([P, S // 16], U16, name="offs_t")
         take_t = sb.tile([P, V // 16], U16, name="take_t")
-        xw = sb.tile([P, T], U32, name="xw", align_bytes=64)
+        xw = rows.tile([P, T], U32, name="xw", align_bytes=64, offset=0)
         xs = sb.tile([P, T], U8, name="xs", align_bytes=64)
         w2s = sb.tile([P, N], U8, name="w2s", align_bytes=64)
         xsp = sb.tile([P, S], U8, name="xsp", align_bytes=64)
@@ -72,18 +73,18 @@ def tile_picked_modtrue_silu_po_kernel(
         for q in range(QUADS):
             nc.scalar.dma_start(xsp[32 * q : 32 * q + 4, :].bitcast(I32), xsg[32 * q : 32 * q + 32 : 8, :].bitcast(I32))
 
-        w1c = sb.tile([P, H], U32, name="w1c", align_bytes=64)
-        w1s = sb.tile([P, H], U8, name="w1s", align_bytes=64)
         w1g = sb.tile([P, H * PACK], BF16, name="w1g", align_bytes=64)
-        dealt = w1g[:].rearrange("p (t m j) -> p m j t", t=PACK, j=PACK)
-        plain = w1raw[:].rearrange("p (j m t) -> p m j t", j=PACK, t=PACK)
+        dealt = w1g[:].rearrange("p (e u m j) -> p m j u e", e=2, u=2, j=PACK)
+        plain = w1raw[:].rearrange("p (j m u e) -> p m j u e", j=PACK, u=2, e=2)
         nc.vector.tensor_copy(dealt, plain)
         gate = late.tile([P, V], F32, name="gate", align_bytes=64, offset=0)
         nc.sync.dma_start(gate[:], wt.rearrange("(p j) v -> p j v", j=PACK)[:, 0, :])
         w2w = late.tile([P, 2 * N], U8, name="w2w", align_bytes=64, offset=4 * V)
         nc.sync.dma_start(w2w[:].bitcast(I32), w2_words[0].bitcast(I32))
 
-        nc.vector.quantize_mx(out=w1c[:].bitcast(FP8X4), scales=w1s[:], in_=w1g[:])
+        w1s = [sb.tile([P, 2 * P], U8, name=f"w1s{e}", align_bytes=64) for e in range(2)]
+        w1c = [sb.tile([P, 2 * P], U32, name="w1c0", align_bytes=64)]
+        nc.vector.quantize_mx(out=w1c[0][:].bitcast(FP8X4), scales=w1s[0][:], in_=w1g[:, : 2 * H])
 
         half = 2 * CH
         halves = [slice(0, half), slice(half, S)]
@@ -96,12 +97,16 @@ def tile_picked_modtrue_silu_po_kernel(
         for q in range(QUADS):
             nc.sync.dma_start(w2sp[32 * q : 32 * q + 4, :].bitcast(I32), w2sd[32 * q : 32 * q + 32 : 8, :].bitcast(I32))
 
+        w1c.append(rows.tile([P, 2 * P], U32, name="w1c1", align_bytes=64, offset=0))
+        nc.vector.quantize_mx(out=w1c[1][:].bitcast(FP8X4), scales=w1s[1][:], in_=w1g[:, 2 * H :])
+
         def layer1(t, tok, bank):
-            cols = slice(P * t, P * (t + 1))
+            u, e = divmod(t, 2)
+            cols = slice(P * u, P * (u + 1))
             width = tok.stop - tok.start
             acc = ps.tile([P, width], F32, name=f"y_acc{bank}", tag=f"bank{bank}")
             nc.tensor.matmul_mx(
-                out=acc[:], lhsT=w1c[:, cols].bitcast(FP8X4), lhsT_scale=w1s[:, cols],
+                out=acc[:], lhsT=w1c[e][:, cols].bitcast(FP8X4), lhsT_scale=w1s[e][:, cols],
                 rhs=xwg[:, tok].bitcast(FP8X4), rhs_scale=xsp[:, tok], start=True, stop=True,
             )
             return acc

@@ -42,14 +42,14 @@ def tile_picked_modtrue_silu_po_kernel(
 
         offs_t = sb.tile([P, S // 16], U16, name="offs_t")
         take_t = sb.tile([P, V // 16], U16, name="take_t")
-        xw = rows.tile([P, T], U32, name="xw", align_bytes=64, offset=0)
-        xs = sb.tile([P, T], U8, name="xs", align_bytes=64)
-        w2s = sb.tile([P, N], U8, name="w2s", align_bytes=64)
-        xsp = sb.tile([P, S], U8, name="xsp", align_bytes=64)
-        w2sp = sb.tile([P, N], U8, name="w2sp", align_bytes=64)
+        xw = rows.tile([P, T], U32, name="xw", align_bytes=256, offset=0)
+        xs = sb.tile([P, T], U8, name="xs", align_bytes=256)
+        w2s = sb.tile([P, N], U8, name="w2s", align_bytes=256)
+        xsp = sb.tile([P, S], U8, name="xsp", align_bytes=256)
+        w2sp = sb.tile([P, N], U8, name="w2sp", align_bytes=256)
         warm_in = sb.tile([P, 8], F32, name="warm_in")
         warm_out = sb.tile([P, 8], F32, name="warm_out")
-        w1raw = late.tile([P, PACK * H], F32, name="w1raw", align_bytes=64, offset=0)
+        w1raw = late.tile([P, PACK * H], F32, name="w1raw", align_bytes=256, offset=0)
 
         nc.vector.memset(xs[:].bitcast(I32), 0)
         nc.vector.memset(w2s[:].bitcast(I32), 0)
@@ -68,36 +68,36 @@ def tile_picked_modtrue_silu_po_kernel(
         nc.sync.dma_start(w2s[0:P:8, :].bitcast(I32), w2_scales[0].bitcast(I32))
         nc.sync.dma_start(take_t[:], take)
 
-        xsg = sb.tile([P, S], U8, name="xsg", align_bytes=64)
+        xsg = sb.tile([P, S], U8, name="xsg", align_bytes=256)
         nc.vector.tensor_copy(xsg[:], xs[:].indirect(offs_t[:]))
         for q in range(QUADS):
             nc.scalar.dma_start(xsp[32 * q : 32 * q + 4, :].bitcast(I32), xsg[32 * q : 32 * q + 32 : 8, :].bitcast(I32))
 
-        w1g = sb.tile([P, H * PACK], BF16, name="w1g", align_bytes=64)
+        w1g = sb.tile([P, H * PACK], BF16, name="w1g", align_bytes=256)
         dealt = w1g[:].rearrange("p (e u m j) -> p m j u e", e=2, u=2, j=PACK)
         plain = w1raw[:].rearrange("p (j m u e) -> p m j u e", j=PACK, u=2, e=2)
         nc.vector.tensor_copy(dealt, plain)
-        gate = late.tile([P, V], F32, name="gate", align_bytes=64, offset=0)
+        gate = late.tile([P, V], F32, name="gate", align_bytes=256, offset=0)
         nc.sync.dma_start(gate[:], wt.rearrange("(p j) v -> p j v", j=PACK)[:, 0, :])
-        w2w = late.tile([P, 2 * N], U8, name="w2w", align_bytes=64, offset=4 * V)
+        w2w = late.tile([P, 2 * N], U8, name="w2w", align_bytes=256, offset=4 * V)
         nc.sync.dma_start(w2w[:].bitcast(I32), w2_words[0].bitcast(I32))
 
-        w1s = [sb.tile([P, 2 * P], U8, name=f"w1s{e}", align_bytes=64) for e in range(2)]
-        w1c = [sb.tile([P, 2 * P], U32, name="w1c0", align_bytes=64)]
+        w1s = [sb.tile([P, 2 * P], U8, name=f"w1s{e}", align_bytes=256) for e in range(2)]
+        w1c = [sb.tile([P, 2 * P], U32, name="w1c0", align_bytes=256)]
         nc.vector.quantize_mx(out=w1c[0][:].bitcast(FP8X4), scales=w1s[0][:], in_=w1g[:, : 2 * H])
 
         half = 2 * CH
         halves = [slice(0, half), slice(half, S)]
-        xwg = sb.tile([P, S], U32, name="xwg", align_bytes=64)
+        xwg = sb.tile([P, S], U32, name="xwg", align_bytes=256)
         for h in range(2):
             nc.vector.tensor_copy(xwg[:, halves[h]], xw[:].indirect(offs_t[:, h * half // 16 : (h + 1) * half // 16]))
 
-        w2sd = sb.tile([P, N], U8, name="w2sd", align_bytes=64)
+        w2sd = sb.tile([P, N], U8, name="w2sd", align_bytes=256)
         nc.vector.tensor_copy(w2sd[:].rearrange("p (t m) -> p t m", t=PACK), w2s[:].rearrange("p (m t) -> p t m", t=PACK))
         for q in range(QUADS):
             nc.sync.dma_start(w2sp[32 * q : 32 * q + 4, :].bitcast(I32), w2sd[32 * q : 32 * q + 32 : 8, :].bitcast(I32))
 
-        w1c.append(rows.tile([P, 2 * P], U32, name="w1c1", align_bytes=64, offset=0))
+        w1c.append(rows.tile([P, 2 * P], U32, name="w1c1", align_bytes=256, offset=0))
         nc.vector.quantize_mx(out=w1c[1][:].bitcast(FP8X4), scales=w1s[1][:], in_=w1g[:, 2 * H :])
 
         def layer1(t, tok, bank):
@@ -111,12 +111,12 @@ def tile_picked_modtrue_silu_po_kernel(
             )
             return acc
 
-        z = {t: sb.tile([P, S], F32, name=f"z{t}", align_bytes=64) for t in (first, second, last)}
-        zq = [sb.tile([P, n, PACK], BF16, name=f"zq{h}", align_bytes=64) for h, n in enumerate((half, CH, CH))]
-        zp = sb.tile([P, PACK, half], F32, name="zp", align_bytes=64)
-        act = {t: sb.tile([P, V], F32, name=f"a{t}", align_bytes=64) for t in ORDER}
-        picked = {t: sb.tile([P, V], F32, name=f"g{t}", align_bytes=64) for t in (second, third)}
-        picked[last] = words.tile([P, V], F32, name="g_last", align_bytes=64, offset=0)
+        z = {t: sb.tile([P, S], F32, name=f"z{t}", align_bytes=256) for t in (first, second, last)}
+        zq = [sb.tile([P, n, PACK], BF16, name=f"zq{h}", align_bytes=256) for h, n in enumerate((half, CH, CH))]
+        zp = sb.tile([P, PACK, half], F32, name="zp", align_bytes=256)
+        act = {t: sb.tile([P, V], F32, name=f"a{t}", align_bytes=256) for t in ORDER}
+        picked = {t: sb.tile([P, V], F32, name=f"g{t}", align_bytes=256) for t in (second, third)}
+        picked[last] = words.tile([P, V], F32, name="g_last", align_bytes=256, offset=0)
 
         def gather(t):
             nc.scalar.activation(picked[t][:], z[t][:].indirect(take_t[:]), COPY)
@@ -135,7 +135,7 @@ def tile_picked_modtrue_silu_po_kernel(
 
         lists = [slice(0, V // 32), slice(V // 32, V // 16)]
         picks = [slice(0, V // 2), slice(V // 2, V)]
-        lead_act = reuse.tile([P, S], F32, name="lead_act", align_bytes=64, offset=0)
+        lead_act = reuse.tile([P, S], F32, name="lead_act", align_bytes=256, offset=0)
         for h in range(2):
             lead = layer1(first, halves[h], 2 * h)
             follow = layer1(second, halves[h], 2 * h + 1)
@@ -146,7 +146,7 @@ def tile_picked_modtrue_silu_po_kernel(
         nc.scalar.activation(act[first][:, picks[1]], lead_act[:].indirect(take_t[:, lists[1]]), COPY)
         gather(second)
         scatter(first)
-        z[third] = reuse.tile([P, S], F32, name="z_third", align_bytes=64, offset=0)
+        z[third] = reuse.tile([P, S], F32, name="z_third", align_bytes=256, offset=0)
         nc.scalar.copy(z[third][:], layer1(third, slice(0, S), 4)[:])
         silu(second)
         scatter(second)
@@ -158,7 +158,7 @@ def tile_picked_modtrue_silu_po_kernel(
         weave_low(nc.scalar.copy, first, 0, half)
         silu(last)
         weave_low(nc.scalar.copy, second, 0, half)
-        w2wd = words.tile([P, 2 * N], U8, name="w2wd", align_bytes=64, offset=0)
+        w2wd = words.tile([P, 2 * N], U8, name="w2wd", align_bytes=256, offset=0)
         nc.scalar.copy(
             w2wd[:].bitcast(U16).rearrange("p (t m) -> p t m", t=PACK), w2w[:].bitcast(U16).rearrange("p (m t) -> p t m", t=PACK)
         )
@@ -168,8 +168,8 @@ def tile_picked_modtrue_silu_po_kernel(
         weave_high(nc.scalar.copy, third)
         scatter(last)
 
-        zc = [sb.tile([P, half], U32, name=f"zc{h}", align_bytes=64) for h in range(2)]
-        zs = [sb.tile([P, half], U8, name=f"zs{h}", align_bytes=64) for h in range(2)]
+        zc = [sb.tile([P, half], U32, name=f"zc{h}", align_bytes=256) for h in range(2)]
+        zs = [sb.tile([P, half], U8, name=f"zs{h}", align_bytes=256) for h in range(2)]
 
         for c in range(2):
             weave_low(nc.vector.tensor_copy, last, c * CH, (c + 1) * CH)
@@ -190,11 +190,11 @@ def tile_picked_modtrue_silu_po_kernel(
                 out=zc[1][:, cols].bitcast(FP8X4), scales=zs[1][:, cols], in_=zq[1 + c][:].rearrange("p n j -> p (n j)")
             )
 
-        ow = sb.tile([P, S], U32, name="ow", align_bytes=64)
-        osc = sb.tile([P, S], U8, name="osc", align_bytes=64)
+        ow = sb.tile([P, S], U32, name="ow", align_bytes=256)
+        osc = sb.tile([P, S], U8, name="osc", align_bytes=256)
         out_rows = out_0.rearrange("(p t) j -> p t j", t=PACK)
-        o32 = sb.tile([P, PACK, S], F32, name="o32", align_bytes=64)
-        oq = [sb.tile([P, CH * PACK], BF16, name=f"oq{k}", align_bytes=64) for k in range(NCH)]
+        o32 = sb.tile([P, PACK, S], F32, name="o32", align_bytes=256)
+        oq = [sb.tile([P, CH * PACK], BF16, name=f"oq{k}", align_bytes=256) for k in range(NCH)]
         banks = []
 
         def product(planes, lo, hi):

from contextlib import ExitStack

import concourse.mybir as mybir

K, T, S, V, H, N = 512, 2048, 512, 256, 512, 512
FLOPS = 2 * K * H * S + 2 * H * N * S
BYTES = K * T + 16 * T + 4 * K * H + 4 * 8 * V + H * N // 2 + 16 * N + 2 * 128 * (S + V) // 16 + 4 * N * S + N * S + 16 * S

F32 = mybir.dt.float32
BF16 = mybir.dt.bfloat16
I32 = mybir.dt.int32
U32 = mybir.dt.uint32
U16 = mybir.dt.uint16
U8 = mybir.dt.uint8
FP8X4 = mybir.dt.float8_e4m3fn_x4
FP4X4 = mybir.dt.float4_e2m1fn_x4
SILU = mybir.ActivationFunctionType.Silu
COPY = mybir.ActivationFunctionType.Copy
MULT = mybir.AluOpType.mult

P = 128
PACK = 4
QUADS = 4
CH = 128
NCH = S // CH
ORDER = (2, 0, 1, 3)
W_HEAD = 3 * PACK * H // 8


def tile_picked_modtrue_silu_po_kernel(
    tc, x_words, x_scales, w1, wt, w2_words, w2_scales, offs, take, out_0, out_1, out_2
):
    nc = tc.nc
    with ExitStack() as ctx:
        sb = ctx.enter_context(tc.tile_pool(name="sb", bufs=1))
        reuse = ctx.enter_context(tc.tile_pool(name="reuse", bufs=1))
        late = ctx.enter_context(tc.tile_pool(name="late", bufs=1))
        words = ctx.enter_context(tc.tile_pool(name="words", bufs=1))
        rows = ctx.enter_context(tc.tile_pool(name="rows", bufs=1))
        ps = ctx.enter_context(tc.psum_pool(name="ps", bufs=1))
        first, second, third, last = ORDER

        offs_t = sb.tile([P, S // 16], U16, name="offs_t")
        take_t = sb.tile([P, V // 16], U16, name="take_t")
        xw = rows.tile([P, T], U32, name="xw", align_bytes=256, offset=0)
        xs = sb.tile([P, T], U8, name="xs", align_bytes=256)
        w2s = sb.tile([P, N], U8, name="w2s", align_bytes=256)
        xsp = sb.tile([P, S], U8, name="xsp", align_bytes=256)
        w2sp = sb.tile([P, N], U8, name="w2sp", align_bytes=256)
        warm_in = sb.tile([P, 8], F32, name="warm_in")
        warm_out = sb.tile([P, 8], F32, name="warm_out")
        w1raw = late.tile([P, PACK * H], F32, name="w1raw", align_bytes=256, offset=0)

        nc.vector.memset(xs[:].bitcast(I32), 0)
        nc.vector.memset(w2s[:].bitcast(I32), 0)
        nc.vector.memset(xsp[:].bitcast(I32), 0)
        nc.vector.memset(w2sp[:].bitcast(I32), 0)
        nc.vector.memset(warm_in[:], 0.0)
        nc.scalar.activation(warm_out[:], warm_in[:], SILU)

        x_rows = x_words[0].rearrange("p c r -> p (c r)").bitcast(I32)
        w1_rows = w1.rearrange("(p j) c -> p (j c)", j=PACK)
        nc.sync.dma_start(w1raw[:, :W_HEAD], w1_rows[:, :W_HEAD])
        nc.sync.dma_start(offs_t[:], offs)
        nc.sync.dma_start(xs[0:P:8, :].bitcast(I32), x_scales[0].bitcast(I32))
        nc.sync.dma_start(w1raw[:, W_HEAD:], w1_rows[:, W_HEAD:])
        nc.sync.dma_start(xw[:].bitcast(I32), x_rows)
        nc.sync.dma_start(w2s[0:P:8, :].bitcast(I32), w2_scales[0].bitcast(I32))
        nc.sync.dma_start(take_t[:], take)

        xsg = sb.tile([P, S], U8, name="xsg", align_bytes=256)
        nc.vector.tensor_copy(xsg[:], xs[:].indirect(offs_t[:]))
        for q in range(QUADS):
            nc.scalar.dma_start(xsp[32 * q : 32 * q + 4, :].bitcast(I32), xsg[32 * q : 32 * q + 32 : 8, :].bitcast(I32))

        w1g = sb.tile([P, H * PACK], BF16, name="w1g", align_bytes=256)
        dealt = w1g[:].rearrange("p (e u m j) -> p m j u e", e=2, u=2, j=PACK)
        plain = w1raw[:].rearrange("p (j m u e) -> p m j u e", j=PACK, u=2, e=2)
        nc.vector.tensor_copy(dealt, plain)
        gate = late.tile([P, V], F32, name="gate", align_bytes=256, offset=0)
        nc.sync.dma_start(gate[:], wt.rearrange("(p j) v -> p j v", j=PACK)[:, 0, :])
        w2w = late.tile([P, 2 * N], U8, name="w2w", align_bytes=256, offset=4 * V)
        nc.sync.dma_start(w2w[:].bitcast(I32), w2_words[0].bitcast(I32))

        w1s = [sb.tile([P, 2 * P], U8, name=f"w1s{e}", align_bytes=256) for e in range(2)]
        w1c = [sb.tile([P, 2 * P], U32, name="w1c0", align_bytes=256)]
        nc.vector.quantize_mx(out=w1c[0][:].bitcast(FP8X4), scales=w1s[0][:], in_=w1g[:, : 2 * H])

        half = 2 * CH
        halves = [slice(0, half), slice(half, S)]
        xwg = sb.tile([P, S], U32, name="xwg", align_bytes=256)
        for h in range(2):
            nc.vector.tensor_copy(xwg[:, halves[h]], xw[:].indirect(offs_t[:, h * half // 16 : (h + 1) * half // 16]))

        w2sd = sb.tile([P, N], U8, name="w2sd", align_bytes=256)
        nc.vector.tensor_copy(w2sd[:].rearrange("p (t m) -> p t m", t=PACK), w2s[:].rearrange("p (m t) -> p t m", t=PACK))
        for q in range(QUADS):
            nc.sync.dma_start(w2sp[32 * q : 32 * q + 4, :].bitcast(I32), w2sd[32 * q : 32 * q + 32 : 8, :].bitcast(I32))

        w1c.append(rows.tile([P, 2 * P], U32, name="w1c1", align_bytes=256, offset=0))
        nc.vector.quantize_mx(out=w1c[1][:].bitcast(FP8X4), scales=w1s[1][:], in_=w1g[:, 2 * H :])

        def layer1(t, tok, bank):
            u, e = divmod(t, 2)
            cols = slice(P * u, P * (u + 1))
            width = tok.stop - tok.start
            acc = ps.tile([P, width], F32, name=f"y_acc{bank}", tag=f"bank{bank}")
            nc.tensor.matmul_mx(
                out=acc[:], lhsT=w1c[e][:, cols].bitcast(FP8X4), lhsT_scale=w1s[e][:, cols],
                rhs=xwg[:, tok].bitcast(FP8X4), rhs_scale=xsp[:, tok], start=True, stop=True,
            )
            return acc

        z = {t: sb.tile([P, S], F32, name=f"z{t}", align_bytes=256) for t in (first, second, last)}
        zq = [sb.tile([P, n, PACK], BF16, name=f"zq{h}", align_bytes=256) for h, n in enumerate((half, CH, CH))]
        zp = sb.tile([P, PACK, half], F32, name="zp", align_bytes=256)
        act = {t: sb.tile([P, V], F32, name=f"a{t}", align_bytes=256) for t in ORDER}
        picked = {t: sb.tile([P, V], F32, name=f"g{t}", align_bytes=256) for t in (second, third)}
        picked[last] = words.tile([P, V], F32, name="g_last", align_bytes=256, offset=0)

        def gather(t):
            nc.scalar.activation(picked[t][:], z[t][:].indirect(take_t[:]), COPY)

        def silu(t):
            nc.scalar.activation(act[t][:], picked[t][:], SILU)

        def scatter(t):
            nc.vector.tensor_tensor(z[t][:].indirect(take_t[:]), act[t][:], gate[:], MULT)

        def weave_low(eng, t, lo, hi):
            eng(zq[0][:, lo:hi, t], z[t][:, lo:hi])

        def weave_high(eng, t):
            eng(zp[:, t, :], z[t][:, half:])

        lists = [slice(0, V // 32), slice(V // 32, V // 16)]
        picks = [slice(0, V // 2), slice(V // 2, V)]
        lead_act = reuse.tile([P, S], F32, name="lead_act", align_bytes=256, offset=0)
        for h in range(2):
            lead = layer1(first, halves[h], 2 * h)
            follow = layer1(second, halves[h], 2 * h + 1)
            nc.scalar.activation(lead_act[:, halves[h]], lead[:], SILU)
            nc.scalar.copy(z[first][:, halves[h]], lead[:])
            nc.vector.tensor_copy(z[second][:, halves[h]], follow[:])
        nc.vector.tensor_copy(act[first][:, picks[0]], lead_act[:].indirect(take_t[:, lists[0]]))
        nc.scalar.activation(act[first][:, picks[1]], lead_act[:].indirect(take_t[:, lists[1]]), COPY)
        gather(second)
        scatter(first)
        z[third] = reuse.tile([P, S], F32, name="z_third", align_bytes=256, offset=0)
        nc.scalar.copy(z[third][:], layer1(third, slice(0, S), 4)[:])
        silu(second)
        scatter(second)
        gather(third)
        nc.scalar.copy(z[last][:], layer1(last, slice(0, S), 5)[:])
        silu(third)
        scatter(third)
        gather(last)
        weave_low(nc.scalar.copy, first, 0, half)
        silu(last)
        weave_low(nc.scalar.copy, second, 0, half)
        w2wd = words.tile([P, 2 * N], U8, name="w2wd", align_bytes=256, offset=0)
        nc.scalar.copy(
            w2wd[:].bitcast(U16).rearrange("p (t m) -> p t m", t=PACK), w2w[:].bitcast(U16).rearrange("p (m t) -> p t m", t=PACK)
        )
        weave_low(nc.scalar.copy, third, 0, half)
        for t in (first, second):
            weave_high(nc.sync.dma_start, t)
        weave_high(nc.scalar.copy, third)
        scatter(last)

        zc = [sb.tile([P, half], U32, name=f"zc{h}", align_bytes=256) for h in range(2)]
        zs = [sb.tile([P, half], U8, name=f"zs{h}", align_bytes=256) for h in range(2)]

        for c in range(2):
            weave_low(nc.vector.tensor_copy, last, c * CH, (c + 1) * CH)
        for c in range(2):
            cols = slice(c * CH, (c + 1) * CH)
            nc.vector.quantize_mx(
                out=zc[0][:, cols].bitcast(FP8X4), scales=zs[0][:, cols], in_=zq[0][:, cols, :].rearrange("p n j -> p (n j)")
            )
        weave_high(nc.scalar.copy, last)
        for c in range(2):
            nc.vector.tensor_copy(
                zq[1 + c][:].rearrange("p (n i) t -> p n t i", i=4),
                zp[:, :, c * CH : (c + 1) * CH].rearrange("p t (n i) -> p n t i", i=4),
            )
        for c in range(2):
            cols = slice(c * CH, (c + 1) * CH)
            nc.vector.quantize_mx(
                out=zc[1][:, cols].bitcast(FP8X4), scales=zs[1][:, cols], in_=zq[1 + c][:].rearrange("p n j -> p (n j)")
            )

        ow = sb.tile([P, S], U32, name="ow", align_bytes=256)
        osc = sb.tile([P, S], U8, name="osc", align_bytes=256)
        out_rows = out_0.rearrange("(p t) j -> p t j", t=PACK)
        o32 = sb.tile([P, PACK, S], F32, name="o32", align_bytes=256)
        oq = [sb.tile([P, CH * PACK], BF16, name=f"oq{k}", align_bytes=256) for k in range(NCH)]
        banks = []

        def product(planes, lo, hi):
            h = lo // half
            cols = slice(lo - h * half, hi - h * half)
            nb = len(banks)
            bank = ps.tile([P, len(planes), hi - lo], F32, name=f"o_acc{nb}", tag=f"bank{nb % 8}")
            banks.append(bank)
            for i, t in enumerate(planes):
                nc.tensor.matmul_mx(
                    out=bank[:, i, :], lhsT=w2wd[:, 2 * P * t : 2 * P * (t + 1)].bitcast(FP4X4),
                    lhsT_scale=w2sp[:, P * t : P * (t + 1)],
                    rhs=zc[h][:, cols].bitcast(FP8X4), rhs_scale=zs[h][:, cols], start=True, stop=True,
                )
            nc.scalar.copy(o32[:, planes[0] : planes[-1] + 1, lo:hi], bank[:])

        def store(t0, t1, lo, hi):
            nc.sync.dma_start(out_rows[:, t0:t1, lo:hi], o32[:, t0:t1, lo:hi])

        def regroup(c):
            nc.vector.tensor_copy(
                oq[c][:].rearrange("p (n i t) -> p n t i", i=4, t=PACK),
                o32[:, :, c * CH : (c + 1) * CH].rearrange("p t (n i) -> p n t i", i=4),
            )

        def quantise_out(k):
            cols = slice(k * CH, (k + 1) * CH)
            nc.vector.quantize_mx(out=ow[:, cols].bitcast(FP8X4), scales=osc[:, cols], in_=oq[k][:])

        def store_words(cols):
            nc.sync.dma_start(out_1[0, :, cols, :].rearrange("p c r -> p (c r)").bitcast(I32), ow[:, cols].bitcast(I32))

        product((0,), 0, CH)
        store(0, 1, 0, CH)
        for t in (1, 2, 3):
            product((t,), 0, half)
            store(t, t + 1, 0, half)
        product((0,), CH, half)
        for c in (0, 1):
            regroup(c)
        for c in (0, 1):
            quantise_out(c)
        product((0,), half, S)
        store(0, 1, CH, S)
        product((1,), half, S)
        store(1, 2, half, S)
        store_words(slice(0, half))
        product((2,), half, S)
        product((3,), half, 3 * CH)
        product((3,), 3 * CH, S)
        store(2, 4, half, S)
        for c in (2, 3):
            regroup(c)
        for c in (2, 3):
            quantise_out(c)
        store_words(slice(half, S))
        for q in range(QUADS):
            eng = nc.sync if q % 2 else nc.scalar
            eng.dma_start(out_2[0, 4 * q : 4 * q + 4, :].bitcast(I32), osc[32 * q : 32 * q + 4, :].bitcast(I32))
